import numpy as np
import ml_dtypes


def mxq(x, axis, fmt="e4m3"):
    dtype, down = {"e4m3": (ml_dtypes.float8_e4m3fn, 7), "e5m2": (ml_dtypes.float8_e5m2, 14)}[fmt]
    v = np.moveaxis(np.asarray(x, np.float32).astype(ml_dtypes.bfloat16).astype(np.float64), axis, -1)
    blocks = v.reshape(v.shape[:-1] + (-1, 32))
    amax = np.abs(blocks).max(-1, keepdims=True)
    byte = np.maximum(np.where(amax > 0, np.frexp(amax)[1] - 1 + 127, 0) - down, 1)
    scale = np.exp2(byte - 127.0)
    codes = (blocks / scale).astype(np.float32).astype(dtype).astype(np.float64)
    return np.moveaxis((codes * scale).reshape(v.shape), -1, axis)


WIDE = False


def mx_kscale(k):
    if not WIDE:
        return np.ones(k)
    levels = np.array([24, -24, 12, -12, 0])
    if k % 512:
        return np.exp2(np.random.permutation(np.resize(levels, k // 32))).repeat(32)
    a = np.empty((k // 512, 16))
    for p in range(k // 512):
        a[p, :8] = np.random.permutation(np.resize(levels, 8))
        for g in range(8):
            far = levels[np.abs(levels - a[p, g]) >= 10]
            a[p, g + 8] = far[np.random.randint(len(far))]
    return np.exp2(a.ravel()).repeat(32)


def f64(x):
    return np.asarray(x).astype(np.float64)


def striped(idx):
    return np.tile(idx.reshape(-1, 16).T, (8, 1)).astype(np.uint16)


def unstriped(offs):
    return offs[:16].T.reshape(-1).astype(np.int64)


E2M1 = np.array([0.0, 0.5, 1.0, 1.5, 2.0, 3.0, 4.0, 6.0, -0.0, -0.5, -1.0, -1.5, -2.0, -3.0, -4.0, -6.0])


def pack_weight(w, fmt):
    k, n = w.shape
    w = f64(np.asarray(w, np.float32).astype(ml_dtypes.bfloat16)).reshape(k // 32, 32, n)
    amax = np.abs(w).max(1)
    if fmt == "e4m3":
        byte = np.frexp(amax)[1] - 1 + 127 - 7
    else:
        mant, ex = np.frexp(amax / 6.0)
        byte = np.where(mant > 0.5, ex, ex - 1) + 127
    byte = np.clip(np.where(amax > 0, byte, 1), 1, 254)
    scaled = (w * np.exp2(127.0 - byte)[:, None, :]).reshape(k, n).astype(np.float32)
    by_word = np.ascontiguousarray(scaled.reshape(k // 512, 128, 4, n).transpose(0, 1, 3, 2))
    if fmt == "e4m3":
        words = by_word.astype(ml_dtypes.float8_e4m3fn).view(np.uint8)
    else:
        c = by_word.astype(ml_dtypes.float4_e2m1fn).view(np.uint8) & 0xF
        words = (c[..., 0::2] | (c[..., 1::2] << 4)).reshape(k // 512, 128, 2 * n)
    return np.ascontiguousarray(words), np.ascontiguousarray(byte.astype(np.uint8).reshape(k // 512, 16, n))


def unpack_weight(words, scales, fmt):
    g, _, n = scales.shape
    words = np.ascontiguousarray(words).reshape(g, 128, n, -1)
    if fmt == "e4m3":
        vals = words.view(ml_dtypes.float8_e4m3fn).astype(np.float64)
    else:
        nib = np.empty((g, 128, n, 4), np.uint8)
        nib[..., 0::2] = words & 0xF
        nib[..., 1::2] = words >> 4
        vals = E2M1[nib]
    vals = vals * np.repeat(np.exp2(scales.astype(np.float64) - 127.0), 8, axis=1)[..., None]
    return vals.transpose(0, 1, 3, 2).reshape(g * 512, n)


K, L, R, N, T, J = 512, 512, 512, 256, 2048, 1024


def setup_inputs():
    n = np.random.standard_normal
    s = mx_kscale(K)[:, None]
    s2 = mx_kscale(L)[:, None]
    u = mx_kscale(R)[:, None]
    p_tab = pack_weight(n((K, T)) * s, "e4m3")
    p_tab2 = pack_weight(n((L, T)) * s2, "e4m3")
    p_wa = pack_weight(n((K, R)) / np.sqrt(K) / s * u.T, "e2m1")
    p_wb = pack_weight(n((L, R)) / np.sqrt(L) / s2 * u.T, "e4m3")
    p_en = pack_weight(n((R, N)) / np.sqrt(R) / u, "e2m1")
    return {
        "tab_words": p_tab[0],
        "tab_scales": p_tab[1],
        "tab2_words": p_tab2[0],
        "tab2_scales": p_tab2[1],
        "wa_words": p_wa[0],
        "wa_scales": p_wa[1],
        "wb_words": p_wb[0],
        "wb_scales": p_wb[1],
        "en_words": p_en[0],
        "en_scales": p_en[1],
        "offs": striped(np.random.permutation(T)[:J]),
        "offs2": striped(np.random.permutation(T)[:J]),
    }


def reference(tab_words, tab_scales, tab2_words, tab2_scales, wa_words, wa_scales, wb_words, wb_scales, en_words, en_scales, offs, offs2):
    idx = unstriped(offs)
    idx2 = unstriped(offs2)
    tab_ = unpack_weight(tab_words, tab_scales, "e4m3")[:, idx]
    tab2_ = unpack_weight(tab2_words, tab2_scales, "e4m3")[:, idx2]
    wa_ = unpack_weight(wa_words, wa_scales, "e2m1")
    wb_ = unpack_weight(wb_words, wb_scales, "e4m3")
    z = wa_.T @ tab_ + wb_.T @ tab2_
    h = np.maximum(z, 0.0)
    h_ = mxq(h, 0, "e4m3")
    en_ = unpack_weight(en_words, en_scales, "e2m1")
    y = en_.T @ h_
    return y

@@ -1,0 +1,162 @@
+from contextlib import ExitStack
+
+import concourse.mybir as mybir
+
+K, L, R, N, T, J = 512, 512, 512, 256, 2048, 1024
+FLOPS = 2 * J * (K * R + L * R + R * N)
+
+F32 = mybir.dt.float32
+BF16 = mybir.dt.bfloat16
+I32 = mybir.dt.int32
+U32 = mybir.dt.uint32
+U16 = mybir.dt.uint16
+U8 = mybir.dt.uint8
+E4M3 = mybir.dt.float8_e4m3fn_x4
+E2M1 = mybir.dt.float4_e2m1fn_x4
+RELU = mybir.ActivationFunctionType.Relu
+
+P = 128
+PACK = 4
+CHUNK = 256
+SUB = 128
+ROW2 = 4
+
+
+def tile_list_kg_relu_none_kernel(
+    tc, tab_words, tab_scales, tab2_words, tab2_scales, wa_words, wa_scales, wb_words, wb_scales,
+    en_words, en_scales, offs, offs2, out
+):
+    nc = tc.nc
+    chunks = J // CHUNK
+
+    def load_scales(queue, plane, row0, scales):
+        rows = scales[0].bitcast(I32)
+        for r in range(4):
+            queue.dma_start(out=plane[row0 + r : P : 32], in_=rows[r:16:4, :])
+
+    with ExitStack() as ctx:
+        keep = ctx.enter_context(tc.tile_pool(name="keep", bufs=1))
+        zps = ctx.enter_context(tc.psum_pool(name="zps", bufs=4))
+        yps = ctx.enter_context(tc.psum_pool(name="yps", bufs=3))
+
+        list1 = keep.tile([P, J // 16], U16, name="list1")
+        list2 = keep.tile([P, J // 16], U16, name="list2")
+        tab1_w = keep.tile([P, T], I32, name="tab1_w", align_bytes=64)
+        tab2_w = keep.tile([P, T], I32, name="tab2_w", align_bytes=64)
+        tab1_s = keep.tile([P, T // 4], I32, name="tab1_s", align_bytes=64)
+        tab2_s = keep.tile([P, T // 4], I32, name="tab2_s", align_bytes=64)
+        wa_raw = keep.tile([P, R // 2], I32, name="wa_raw", align_bytes=64)
+        wb_raw = keep.tile([P, R], I32, name="wb_raw", align_bytes=64)
+        ws_raw = keep.tile([P, R // 4], I32, name="ws_raw", align_bytes=64)
+        wa_w = keep.tile([P, R], U16, name="wa_w", align_bytes=64)
+        wb_w = keep.tile([P, R], I32, name="wb_w", align_bytes=64)
+        w_s = keep.tile([P, R], U8, name="w_s", align_bytes=64)
+        en_w = keep.tile([P, N // 2], I32, name="en_w", align_bytes=64)
+        en_s = keep.tile([P, N // 4], I32, name="en_s", align_bytes=64)
+        warm = keep.tile([P, 8], F32, name="warm")
+        warm_out = keep.tile([P, 8], F32, name="warm_out")
+
+        nc.vector.memset(tab1_s[:], 0)
+        nc.vector.memset(warm[:], 0.0)
+        nc.vector.memset(tab2_s[:], 0)
+        nc.vector.memset(ws_raw[:], 0)
+        nc.vector.memset(en_s[:], 0)
+
+        nc.sync.dma_start(list1[:], offs)
+        nc.gpsimd.dma_start(out=tab1_w[:], in_=tab_words[0].rearrange("p t i -> p (t i)").bitcast(I32))
+        nc.gpsimd.dma_start(out=tab2_w[:], in_=tab2_words[0].rearrange("p t i -> p (t i)").bitcast(I32))
+        nc.gpsimd.dma_start(out=en_w[:], in_=en_words[0].bitcast(I32))
+        load_scales(nc.sync, tab1_s[:], 0, tab_scales)
+        nc.sync.dma_start(list2[:], offs2)
+        nc.scalar.dma_start(out=wa_raw[:], in_=wa_words[0].bitcast(I32))
+        nc.scalar.dma_start(out=wb_raw[:], in_=wb_words[0].rearrange("p r i -> p (r i)").bitcast(I32))
+        load_scales(nc.sync, tab2_s[:], ROW2, tab2_scales)
+        load_scales(nc.sync, ws_raw[:], 0, wa_scales)
+        load_scales(nc.sync, ws_raw[:], ROW2, wb_scales)
+        load_scales(nc.sync, en_s[:], 0, en_scales)
+
+        nc.scalar.activation(out=warm_out[:], in_=warm[:], func=RELU)
+
+        g1_s = keep.tile([P, J], U8, name="g1_s", align_bytes=64)
+        g1_w = [keep.tile([P, CHUNK], U32, name="g1_w%d" % c, align_bytes=64) for c in range(chunks)]
+        g2_w = [keep.tile([P, CHUNK], U32, name="g2_w%d" % c, align_bytes=64) for c in range(chunks)]
+        g2_s = [keep.tile([P, CHUNK], U8, name="g2_s%d" % c, align_bytes=64) for c in range(chunks)]
+        h = [keep.tile([P, CHUNK, PACK], BF16, name="h%d" % c, align_bytes=64) for c in range(chunks)]
+        h_w = [keep.tile([P, CHUNK], U32, name="h_w%d" % c, align_bytes=64) for c in range(chunks)]
+        h_s = [keep.tile([P, CHUNK], U8, name="h_s%d" % c, align_bytes=64) for c in range(chunks)]
+
+        def entries(lst, c):
+            return lst[:, c * (CHUNK // 16) : (c + 1) * (CHUNK // 16)]
+
+        def gather(c):
+            nc.vector.tensor_copy(g1_w[c][:], tab1_w[:].bitcast(U32).indirect(entries(list1, c)))
+            nc.vector.tensor_copy(g2_s[c][:], tab2_s[:].bitcast(U8).indirect(entries(list2, c)))
+            nc.vector.tensor_copy(g2_w[c][:], tab2_w[:].bitcast(U32).indirect(entries(list2, c)))
+
+        def project(c, s, on_vector):
+            cols = slice(s * SUB, (s + 1) * SUB)
+            j0 = c * CHUNK + s * SUB
+            z = zps.tile([P, PACK, SUB], F32, name="z")
+            for t in range(PACK):
+                rows = slice(t * P, (t + 1) * P)
+                nc.tensor.matmul_mx(
+                    out=z[:, t, :], lhsT=wa_w[:, rows].bitcast(E2M1), lhsT_scale=w_s[:, rows],
+                    rhs=g1_w[c][:, cols].bitcast(E4M3), rhs_scale=g1_s[:, j0 : j0 + SUB],
+                    start=True, stop=False,
+                )
+                nc.tensor.matmul_mx(
+                    out=z[:, t, :], lhsT=wb_w[:, rows].bitcast(E4M3), lhsT_scale=w_s[ROW2:P, rows],
+                    rhs=g2_w[c][:, cols].bitcast(E4M3), rhs_scale=g2_s[c][ROW2:P, cols],
+                    start=False, stop=True,
+                )
+            src = z[:].rearrange("p t j -> p j t")
+            if on_vector:
+                nc.vector.tensor_scalar_max(h[c][:, cols, :], src, 0.0)
+            else:
+                nc.scalar.activation(out=h[c][:, cols, :], in_=src, func=RELU)
+
+        def score(c, lo, width, on_vector, queue):
+            cols = slice(lo, lo + width)
+            nc.vector.quantize_mx(
+                out=h_w[c][:, cols].bitcast(E4M3), scales=h_s[c][:, cols],
+                in_=h[c][:, cols, :].rearrange("p j t -> p (j t)"),
+            )
+            y = yps.tile([P, 2, width], F32, name="y")
+            for u in range(2):
+                nc.tensor.matmul_mx(
+                    out=y[:, u, :], lhsT=en_w[:, u * 64 : (u + 1) * 64].bitcast(E2M1),
+                    lhsT_scale=en_s[:].bitcast(U8)[:, u * P : (u + 1) * P],
+                    rhs=h_w[c][:, cols].bitcast(E4M3), rhs_scale=h_s[c][:, cols],
+                    start=True, stop=True,
+                )
+            res = keep.tile([P, 2, width], F32, name="res%d_%d" % (c, lo))
+            if on_vector:
+                nc.vector.tensor_copy(res[:], y[:])
+            else:
+                nc.scalar.copy(res[:], y[:])
+            j0 = c * CHUNK + lo
+            queue.dma_start(out=out.rearrange("(u p) j -> p u j", p=P)[:, :, j0 : j0 + width], in_=res[:])
+
+        nc.vector.tensor_copy(g1_s[:], tab1_s[:].bitcast(U8).indirect(list1[:]))
+        nc.vector.tensor_copy(
+            wa_w[:].rearrange("p (t m) -> p t m", t=PACK),
+            wa_raw[:].bitcast(U16).rearrange("p (m t) -> p t m", t=PACK),
+        )
+        nc.vector.tensor_copy(
+            wb_w[:].rearrange("p (t m) -> p m t", t=PACK),
+            wb_raw[:].rearrange("p (m t) -> p m t", t=PACK),
+        )
+        nc.vector.tensor_copy(
+            w_s[:].rearrange("p (t m) -> p t m", t=PACK),
+            ws_raw[:].bitcast(U8).rearrange("p (m t) -> p t m", t=PACK),
+        )
+
+        last = chunks - 1
+        for c in range(chunks):
+            gather(c)
+            project(c, 0, False)
+            project(c, 1, c == last)
+            if c > 0:
+                score(c - 1, 0, CHUNK, False, nc.sync)
+        score(last, 0, SUB, False, nc.sync)
+        score(last, SUB, SUB, True, nc.scalar)

@@ -32,11 +32,13 @@ def tile_list_kg_relu_none_kernel(
     def load_scales(queue, plane, row0, scales):
         rows = scales[0].bitcast(I32)
         for r in range(4):
-            queue.dma_start(out=plane[row0 + r : P : 32], in_=rows[r:16:4, :])
+            queue[r % 2].dma_start(out=plane[row0 + r : P : 32], in_=rows[r:16:4, :])
 
     with ExitStack() as ctx:
         keep = ctx.enter_context(tc.tile_pool(name="keep", bufs=1))
+        ring = ctx.enter_context(tc.tile_pool(name="ring", bufs=2))
         zps = ctx.enter_context(tc.psum_pool(name="zps", bufs=4))
+        wps = ctx.enter_context(tc.psum_pool(name="wps", bufs=1))
         yps = ctx.enter_context(tc.psum_pool(name="yps", bufs=3))
 
         list1 = keep.tile([P, J // 16], U16, name="list1")
@@ -58,29 +60,30 @@ def tile_list_kg_relu_none_kernel(
 
         nc.vector.memset(tab1_s[:], 0)
         nc.vector.memset(warm[:], 0.0)
-        nc.vector.memset(tab2_s[:], 0)
         nc.vector.memset(ws_raw[:], 0)
+        nc.vector.memset(tab2_s[:], 0)
         nc.vector.memset(en_s[:], 0)
 
+        both = (nc.sync, nc.scalar)
         nc.sync.dma_start(list1[:], offs)
         nc.gpsimd.dma_start(out=tab1_w[:], in_=tab_words[0].rearrange("p t i -> p (t i)").bitcast(I32))
         nc.gpsimd.dma_start(out=tab2_w[:], in_=tab2_words[0].rearrange("p t i -> p (t i)").bitcast(I32))
         nc.gpsimd.dma_start(out=en_w[:], in_=en_words[0].bitcast(I32))
-        load_scales(nc.sync, tab1_s[:], 0, tab_scales)
+        load_scales(both, tab1_s[:], 0, tab_scales)
         nc.sync.dma_start(list2[:], offs2)
         nc.scalar.dma_start(out=wa_raw[:], in_=wa_words[0].bitcast(I32))
         nc.scalar.dma_start(out=wb_raw[:], in_=wb_words[0].rearrange("p r i -> p (r i)").bitcast(I32))
-        load_scales(nc.sync, tab2_s[:], ROW2, tab2_scales)
-        load_scales(nc.sync, ws_raw[:], 0, wa_scales)
-        load_scales(nc.sync, ws_raw[:], ROW2, wb_scales)
-        load_scales(nc.sync, en_s[:], 0, en_scales)
+        load_scales(both, ws_raw[:], 0, wa_scales)
+        load_scales(both, ws_raw[:], ROW2, wb_scales)
+        load_scales(both, tab2_s[:], ROW2, tab2_scales)
+        load_scales(both, en_s[:], 0, en_scales)
 
         nc.scalar.activation(out=warm_out[:], in_=warm[:], func=RELU)
 
         g1_s = keep.tile([P, J], U8, name="g1_s", align_bytes=64)
-        g1_w = [keep.tile([P, CHUNK], U32, name="g1_w%d" % c, align_bytes=64) for c in range(chunks)]
-        g2_w = [keep.tile([P, CHUNK], U32, name="g2_w%d" % c, align_bytes=64) for c in range(chunks)]
-        g2_s = [keep.tile([P, CHUNK], U8, name="g2_s%d" % c, align_bytes=64) for c in range(chunks)]
+        g1_w = {}
+        g2_w = {}
+        g2_s = keep.tile([P, J], U8, name="g2_s", align_bytes=64)
         h = [keep.tile([P, CHUNK, PACK], BF16, name="h%d" % c, align_bytes=64) for c in range(chunks)]
         h_w = [keep.tile([P, CHUNK], U32, name="h_w%d" % c, align_bytes=64) for c in range(chunks)]
         h_s = [keep.tile([P, CHUNK], U8, name="h_s%d" % c, align_bytes=64) for c in range(chunks)]
@@ -89,8 +92,14 @@ def tile_list_kg_relu_none_kernel(
             return lst[:, c * (CHUNK // 16) : (c + 1) * (CHUNK // 16)]
 
         def gather(c):
+            g1_w[c] = ring.tile([P, CHUNK], U32, name="g1_w", align_bytes=64)
+            g2_w[c] = ring.tile([P, CHUNK], U32, name="g2_w", align_bytes=64)
             nc.vector.tensor_copy(g1_w[c][:], tab1_w[:].bitcast(U32).indirect(entries(list1, c)))
-            nc.vector.tensor_copy(g2_s[c][:], tab2_s[:].bitcast(U8).indirect(entries(list2, c)))
+            if c < 3:
+                hi = J if c == 2 else (c + 1) * CHUNK
+                nc.vector.tensor_copy(
+                    g2_s[:, c * CHUNK : hi], tab2_s[:].bitcast(U8).indirect(list2[:, c * CHUNK // 16 : hi // 16])
+                )
             nc.vector.tensor_copy(g2_w[c][:], tab2_w[:].bitcast(U32).indirect(entries(list2, c)))
 
         def project(c, s, on_vector):
@@ -106,7 +115,7 @@ def tile_list_kg_relu_none_kernel(
                 )
                 nc.tensor.matmul_mx(
                     out=z[:, t, :], lhsT=wb_w[:, rows].bitcast(E4M3), lhsT_scale=w_s[ROW2:P, rows],
-                    rhs=g2_w[c][:, cols].bitcast(E4M3), rhs_scale=g2_s[c][ROW2:P, cols],
+                    rhs=g2_w[c][:, cols].bitcast(E4M3), rhs_scale=g2_s[ROW2:P, j0 : j0 + SUB],
                     start=False, stop=True,
                 )
             src = z[:].rearrange("p t j -> p j t")
@@ -152,11 +161,22 @@ def tile_list_kg_relu_none_kernel(
         )
 
         last = chunks - 1
+        gather(0)
+        gather(1)
+        idle = wps.tile([P, CHUNK], F32, name="idle")
+        for t in range(PACK):
+            rows = slice(t * P, (t + 1) * P)
+            nc.tensor.matmul_mx(
+                out=idle[:], lhsT=wa_w[:, rows].bitcast(E2M1), lhsT_scale=w_s[:, rows],
+                rhs=g1_w[1][:].bitcast(E4M3), rhs_scale=g1_s[:, CHUNK : 2 * CHUNK],
+                start=True, stop=True,
+            )
         for c in range(chunks):
-            gather(c)
-            project(c, 0, False)
-            project(c, 1, c == last)
+            if c > 1:
+                gather(c)
+            project(c, 0, c == last)
+            project(c, 1, False)
             if c > 0:
                 score(c - 1, 0, CHUNK, False, nc.sync)
-        score(last, 0, SUB, False, nc.sync)
-        score(last, SUB, SUB, True, nc.scalar)
+        score(last, 0, SUB, True, nc.sync)
+        score(last, SUB, SUB, False, nc.scalar)

@@ -32,93 +32,105 @@ def tile_list_kg_relu_none_kernel(
     def load_scales(queue, plane, row0, scales):
         rows = scales[0].bitcast(I32)
         for r in range(4):
-            queue[r % 2].dma_start(out=plane[row0 + r : P : 32], in_=rows[r:16:4, :])
+            queue[r % len(queue)].dma_start(out=plane[row0 + r : P : 32], in_=rows[r:16:4, :])
 
     with ExitStack() as ctx:
         keep = ctx.enter_context(tc.tile_pool(name="keep", bufs=1))
-        ring = ctx.enter_context(tc.tile_pool(name="ring", bufs=2))
-        zps = ctx.enter_context(tc.psum_pool(name="zps", bufs=4))
-        wps = ctx.enter_context(tc.psum_pool(name="wps", bufs=1))
+        lay = ctx.enter_context(tc.tile_pool(name="lay", bufs=1))
+        zps = ctx.enter_context(tc.psum_pool(name="zps", bufs=5))
         yps = ctx.enter_context(tc.psum_pool(name="yps", bufs=3))
 
         list1 = keep.tile([P, J // 16], U16, name="list1")
         list2 = keep.tile([P, J // 16], U16, name="list2")
         tab1_w = keep.tile([P, T], I32, name="tab1_w", align_bytes=64)
         tab2_w = keep.tile([P, T], I32, name="tab2_w", align_bytes=64)
-        tab1_s = keep.tile([P, T // 4], I32, name="tab1_s", align_bytes=64)
+        tab1_s = lay.tile([P, T // 4], I32, name="tab1_s", align_bytes=64, offset=12288)
         tab2_s = keep.tile([P, T // 4], I32, name="tab2_s", align_bytes=64)
         wa_raw = keep.tile([P, R // 2], I32, name="wa_raw", align_bytes=64)
-        wb_raw = keep.tile([P, R], I32, name="wb_raw", align_bytes=64)
-        ws_raw = keep.tile([P, R // 4], I32, name="ws_raw", align_bytes=64)
+        wb_raw = keep.tile([P, R], I32, name="wb_raw", tag="early", align_bytes=64)
+        ws_raw = lay.tile([P, R // 4], I32, name="ws_raw", align_bytes=64, offset=8192 + 2048 - 256)
         wa_w = keep.tile([P, R], U16, name="wa_w", align_bytes=64)
         wb_w = keep.tile([P, R], I32, name="wb_w", align_bytes=64)
         w_s = keep.tile([P, R], U8, name="w_s", align_bytes=64)
         en_w = keep.tile([P, N // 2], I32, name="en_w", align_bytes=64)
         en_s = keep.tile([P, N // 4], I32, name="en_s", align_bytes=64)
+        tab1_src = tab_words[0].rearrange("p t i -> p (t i)").bitcast(I32)
+        tab2_src = tab2_words[0].rearrange("p t i -> p (t i)").bitcast(I32)
+        wb_src = wb_words[0].rearrange("p r i -> p (r i)").bitcast(I32)
+        both = (nc.sync, nc.scalar)
+
         warm = keep.tile([P, 8], F32, name="warm")
         warm_out = keep.tile([P, 8], F32, name="warm_out")
-
         nc.vector.memset(tab1_s[:], 0)
         nc.vector.memset(warm[:], 0.0)
         nc.vector.memset(ws_raw[:], 0)
         nc.vector.memset(tab2_s[:], 0)
         nc.vector.memset(en_s[:], 0)
 
-        both = (nc.sync, nc.scalar)
+        nc.scalar.dma_start(out=wb_raw[:], in_=wb_src)
+        nc.sync.dma_start(out=wa_raw[:], in_=wa_words[0].bitcast(I32))
         nc.sync.dma_start(list1[:], offs)
-        nc.gpsimd.dma_start(out=tab1_w[:], in_=tab_words[0].rearrange("p t i -> p (t i)").bitcast(I32))
-        nc.gpsimd.dma_start(out=tab2_w[:], in_=tab2_words[0].rearrange("p t i -> p (t i)").bitcast(I32))
+        nc.gpsimd.dma_start(out=tab1_w[:], in_=tab1_src)
+        nc.gpsimd.dma_start(out=tab2_w[:], in_=tab2_src)
         nc.gpsimd.dma_start(out=en_w[:], in_=en_words[0].bitcast(I32))
         load_scales(both, tab1_s[:], 0, tab_scales)
         nc.sync.dma_start(list2[:], offs2)
-        nc.scalar.dma_start(out=wa_raw[:], in_=wa_words[0].bitcast(I32))
-        nc.scalar.dma_start(out=wb_raw[:], in_=wb_words[0].rearrange("p r i -> p (r i)").bitcast(I32))
+        nc.scalar.activation(out=warm_out[:], in_=warm[:], func=RELU)
         load_scales(both, ws_raw[:], 0, wa_scales)
         load_scales(both, ws_raw[:], ROW2, wb_scales)
         load_scales(both, tab2_s[:], ROW2, tab2_scales)
         load_scales(both, en_s[:], 0, en_scales)
 
-        nc.scalar.activation(out=warm_out[:], in_=warm[:], func=RELU)
-
-        g1_s = keep.tile([P, J], U8, name="g1_s", align_bytes=64)
+        g1_s = keep.tile([P, J], U8, name="g1_s", tag="early", align_bytes=64)
         g1_w = {}
         g2_w = {}
-        g2_s = keep.tile([P, J], U8, name="g2_s", align_bytes=64)
-        h = [keep.tile([P, CHUNK, PACK], BF16, name="h%d" % c, align_bytes=64) for c in range(chunks)]
+        g2_s = {}
+        z = {}
+        first_w = lay.tile([P, 2 * CHUNK], U32, name="first_w", align_bytes=64, offset=8192)
+        first_s = lay.tile([P, 2 * CHUNK], U8, name="first_s", align_bytes=64, offset=8192 + 2048)
+        h = [lay.tile([P, CHUNK, PACK], BF16, name="h%d" % c, align_bytes=64, offset=2048 * c) for c in range(chunks)]
         h_w = [keep.tile([P, CHUNK], U32, name="h_w%d" % c, align_bytes=64) for c in range(chunks)]
         h_s = [keep.tile([P, CHUNK], U8, name="h_s%d" % c, align_bytes=64) for c in range(chunks)]
 
         def entries(lst, c):
             return lst[:, c * (CHUNK // 16) : (c + 1) * (CHUNK // 16)]
 
-        def gather(c):
-            g1_w[c] = ring.tile([P, CHUNK], U32, name="g1_w", align_bytes=64)
-            g2_w[c] = ring.tile([P, CHUNK], U32, name="g2_w", align_bytes=64)
+        def gather1(c):
+            g1_w[c] = lay.tile([P, CHUNK], U32, name="g1_w%d" % c, align_bytes=64, offset=12288 - 960 + 1024 * (c % 3))
             nc.vector.tensor_copy(g1_w[c][:], tab1_w[:].bitcast(U32).indirect(entries(list1, c)))
-            if c < 3:
-                hi = J if c == 2 else (c + 1) * CHUNK
-                nc.vector.tensor_copy(
-                    g2_s[:, c * CHUNK : hi], tab2_s[:].bitcast(U8).indirect(list2[:, c * CHUNK // 16 : hi // 16])
-                )
-            nc.vector.tensor_copy(g2_w[c][:], tab2_w[:].bitcast(U32).indirect(entries(list2, c)))
 
-        def project(c, s, on_vector):
+        def gather2(c):
+            if c >= 2:
+                g2_s[c] = lay.tile([P, CHUNK], U8, name="g2_s%d" % c, align_bytes=64, offset=2048 * (c - 2) + 1024)[:]
+                g2_w[c] = lay.tile([P, CHUNK], U32, name="g2_w%d" % c, align_bytes=64, offset=2048 * (c - 2))[:]
+            else:
+                g2_s[c] = first_s[:, c * CHUNK : (c + 1) * CHUNK]
+                g2_w[c] = first_w[:, c * CHUNK : (c + 1) * CHUNK]
+            nc.vector.tensor_copy(g2_s[c], tab2_s[:].bitcast(U8).indirect(entries(list2, c)))
+            nc.vector.tensor_copy(g2_w[c], tab2_w[:].bitcast(U32).indirect(entries(list2, c)))
+
+        def open_sum(c, s):
             cols = slice(s * SUB, (s + 1) * SUB)
             j0 = c * CHUNK + s * SUB
-            z = zps.tile([P, PACK, SUB], F32, name="z")
+            z[c, s] = zps.tile([P, PACK, SUB], F32, name="z")
             for t in range(PACK):
                 rows = slice(t * P, (t + 1) * P)
                 nc.tensor.matmul_mx(
-                    out=z[:, t, :], lhsT=wa_w[:, rows].bitcast(E2M1), lhsT_scale=w_s[:, rows],
+                    out=z[c, s][:, t, :], lhsT=wa_w[:, rows].bitcast(E2M1), lhsT_scale=w_s[:, rows],
                     rhs=g1_w[c][:, cols].bitcast(E4M3), rhs_scale=g1_s[:, j0 : j0 + SUB],
-                    start=True, stop=False,
+                    start=(t == 0), stop=False,
                 )
+
+        def close_sum(c, s, on_vector):
+            cols = slice(s * SUB, (s + 1) * SUB)
+            for t in range(PACK):
+                rows = slice(t * P, (t + 1) * P)
                 nc.tensor.matmul_mx(
-                    out=z[:, t, :], lhsT=wb_w[:, rows].bitcast(E4M3), lhsT_scale=w_s[ROW2:P, rows],
-                    rhs=g2_w[c][:, cols].bitcast(E4M3), rhs_scale=g2_s[ROW2:P, j0 : j0 + SUB],
-                    start=False, stop=True,
+                    out=z[c, s][:, t, :], lhsT=wb_w[:, rows].bitcast(E4M3), lhsT_scale=w_s[ROW2:P, rows],
+                    rhs=g2_w[c][:, cols].bitcast(E4M3), rhs_scale=g2_s[c][ROW2:P, cols],
+                    start=False, stop=(t == PACK - 1),
                 )
-            src = z[:].rearrange("p t j -> p j t")
+            src = z[c, s][:].rearrange("p t j -> p j t")
             if on_vector:
                 nc.vector.tensor_scalar_max(h[c][:, cols, :], src, 0.0)
             else:
@@ -146,37 +158,46 @@ def tile_list_kg_relu_none_kernel(
             j0 = c * CHUNK + lo
             queue.dma_start(out=out.rearrange("(u p) j -> p u j", p=P)[:, :, j0 : j0 + width], in_=res[:])
 
-        nc.vector.tensor_copy(g1_s[:], tab1_s[:].bitcast(U8).indirect(list1[:]))
-        nc.vector.tensor_copy(
-            wa_w[:].rearrange("p (t m) -> p t m", t=PACK),
-            wa_raw[:].bitcast(U16).rearrange("p (m t) -> p t m", t=PACK),
-        )
-        nc.vector.tensor_copy(
-            wb_w[:].rearrange("p (t m) -> p m t", t=PACK),
-            wb_raw[:].rearrange("p (m t) -> p m t", t=PACK),
-        )
-        nc.vector.tensor_copy(
-            w_s[:].rearrange("p (t m) -> p t m", t=PACK),
-            ws_raw[:].bitcast(U8).rearrange("p (m t) -> p t m", t=PACK),
-        )
-
-        last = chunks - 1
-        gather(0)
-        gather(1)
-        idle = wps.tile([P, CHUNK], F32, name="idle")
-        for t in range(PACK):
-            rows = slice(t * P, (t + 1) * P)
-            nc.tensor.matmul_mx(
-                out=idle[:], lhsT=wa_w[:, rows].bitcast(E2M1), lhsT_scale=w_s[:, rows],
-                rhs=g1_w[1][:].bitcast(E4M3), rhs_scale=g1_s[:, CHUNK : 2 * CHUNK],
-                start=True, stop=True,
+        def deal_wa():
+            nc.vector.tensor_copy(
+                wa_w[:].rearrange("p (t m) -> p t m", t=PACK),
+                wa_raw[:].bitcast(U16).rearrange("p (m t) -> p t m", t=PACK),
             )
+
+        def deal_wb():
+            nc.vector.tensor_copy(
+                wb_w[:].rearrange("p (t m) -> p m t", t=PACK),
+                wb_raw[:].rearrange("p (m t) -> p m t", t=PACK),
+            )
+
+        def deal_scales():
+            nc.vector.tensor_copy(
+                w_s[:].rearrange("p (t m) -> p t m", t=PACK),
+                ws_raw[:].bitcast(U8).rearrange("p (m t) -> p t m", t=PACK),
+            )
+
+        def gather1_scales():
+            nc.vector.tensor_copy(g1_s[:], tab1_s[:].bitcast(U8).indirect(list1[:]))
+
+        deal_wa()
+        deal_wb()
+        gather1_scales()
+        gather1(0)
+        gather1(1)
+        deal_scales()
+        last = chunks - 1
+        for c in range(2):
+            open_sum(c, 0)
+            open_sum(c, 1)
         for c in range(chunks):
-            if c > 1:
-                gather(c)
-            project(c, 0, c == last)
-            project(c, 1, False)
+            gather2(c)
             if c > 0:
                 score(c - 1, 0, CHUNK, False, nc.sync)
+            close_sum(c, 0, c == last)
+            close_sum(c, 1, False)
+            if c + 2 < chunks:
+                gather1(c + 2)
+                open_sum(c + 2, 0)
+                open_sum(c + 2, 1)
         score(last, 0, SUB, True, nc.sync)
         score(last, SUB, SUB, False, nc.scalar)

@@ -44,14 +44,14 @@ def tile_list_kg_relu_none_kernel(
         list2 = keep.tile([P, J // 16], U16, name="list2")
         tab1_w = keep.tile([P, T], I32, name="tab1_w", align_bytes=64)
         tab2_w = keep.tile([P, T], I32, name="tab2_w", align_bytes=64)
-        tab1_s = lay.tile([P, T // 4], I32, name="tab1_s", align_bytes=64, offset=12288)
+        tab1_s = lay.tile([P, T // 4], I32, name="tab1_s", align_bytes=64, offset=13312)
         tab2_s = keep.tile([P, T // 4], I32, name="tab2_s", align_bytes=64)
         wa_raw = keep.tile([P, R // 2], I32, name="wa_raw", align_bytes=64)
         wb_raw = keep.tile([P, R], I32, name="wb_raw", tag="early", align_bytes=64)
-        ws_raw = lay.tile([P, R // 4], I32, name="ws_raw", align_bytes=64, offset=8192 + 2048 - 256)
+        ws_tile = lay.tile([P, 160], I32, name="ws_tile", align_bytes=64, offset=9152)
+        ws_raw = ws_tile[:, 0 : R // 4]
         wa_w = keep.tile([P, R], U16, name="wa_w", align_bytes=64)
         wb_w = keep.tile([P, R], I32, name="wb_w", align_bytes=64)
-        w_s = keep.tile([P, R], U8, name="w_s", align_bytes=64)
         en_w = keep.tile([P, N // 2], I32, name="en_w", align_bytes=64)
         en_s = keep.tile([P, N // 4], I32, name="en_s", align_bytes=64)
         tab1_src = tab_words[0].rearrange("p t i -> p (t i)").bitcast(I32)
@@ -62,32 +62,32 @@ def tile_list_kg_relu_none_kernel(
         warm = keep.tile([P, 8], F32, name="warm")
         warm_out = keep.tile([P, 8], F32, name="warm_out")
         nc.vector.memset(tab1_s[:], 0)
-        nc.vector.memset(warm[:], 0.0)
-        nc.vector.memset(ws_raw[:], 0)
+        nc.vector.memset(ws_raw, 0)
         nc.vector.memset(tab2_s[:], 0)
-        nc.vector.memset(en_s[:], 0)
 
+        nc.scalar.dma_start(out=wa_raw[:], in_=wa_words[0].bitcast(I32))
         nc.scalar.dma_start(out=wb_raw[:], in_=wb_src)
-        nc.sync.dma_start(out=wa_raw[:], in_=wa_words[0].bitcast(I32))
         nc.sync.dma_start(list1[:], offs)
         nc.gpsimd.dma_start(out=tab1_w[:], in_=tab1_src)
-        nc.gpsimd.dma_start(out=tab2_w[:], in_=tab2_src)
         nc.gpsimd.dma_start(out=en_w[:], in_=en_words[0].bitcast(I32))
+        nc.gpsimd.memset(en_s[:], 0)
+        nc.gpsimd.memset(warm[:], 0.0)
+        nc.gpsimd.dma_start(out=tab2_w[:], in_=tab2_src)
         load_scales(both, tab1_s[:], 0, tab_scales)
         nc.sync.dma_start(list2[:], offs2)
-        nc.scalar.activation(out=warm_out[:], in_=warm[:], func=RELU)
-        load_scales(both, ws_raw[:], 0, wa_scales)
-        load_scales(both, ws_raw[:], ROW2, wb_scales)
+        load_scales(both, ws_raw, 0, wa_scales)
+        load_scales(both, ws_raw, ROW2, wb_scales)
         load_scales(both, tab2_s[:], ROW2, tab2_scales)
-        load_scales(both, en_s[:], 0, en_scales)
+        nc.scalar.activation(out=warm_out[:], in_=warm[:], func=RELU)
+        load_scales((nc.sync,), en_s[:], 0, en_scales)
 
         g1_s = keep.tile([P, J], U8, name="g1_s", tag="early", align_bytes=64)
         g1_w = {}
         g2_w = {}
         g2_s = {}
         z = {}
-        first_w = lay.tile([P, 2 * CHUNK], U32, name="first_w", align_bytes=64, offset=8192)
-        first_s = lay.tile([P, 2 * CHUNK], U8, name="first_s", align_bytes=64, offset=8192 + 2048)
+        w_s = lay.tile([P, R], U8, name="w_s", align_bytes=64, offset=14336)
+        mid_w = lay.tile([P, 3 * CHUNK], U32, name="mid_w", align_bytes=64, offset=9728)
         h = [lay.tile([P, CHUNK, PACK], BF16, name="h%d" % c, align_bytes=64, offset=2048 * c) for c in range(chunks)]
         h_w = [keep.tile([P, CHUNK], U32, name="h_w%d" % c, align_bytes=64) for c in range(chunks)]
         h_s = [keep.tile([P, CHUNK], U8, name="h_s%d" % c, align_bytes=64) for c in range(chunks)]
@@ -96,16 +96,16 @@ def tile_list_kg_relu_none_kernel(
             return lst[:, c * (CHUNK // 16) : (c + 1) * (CHUNK // 16)]
 
         def gather1(c):
-            g1_w[c] = lay.tile([P, CHUNK], U32, name="g1_w%d" % c, align_bytes=64, offset=12288 - 960 + 1024 * (c % 3))
-            nc.vector.tensor_copy(g1_w[c][:], tab1_w[:].bitcast(U32).indirect(entries(list1, c)))
+            if c > 0:
+                g1_w[c] = mid_w[:, (c - 1) * CHUNK : c * CHUNK]
+            else:
+                g1_w[c] = lay.tile([P, CHUNK], U32, name="g1_w%d" % c, align_bytes=64, offset=13312)[:]
+            nc.vector.tensor_copy(g1_w[c], tab1_w[:].bitcast(U32).indirect(entries(list1, c)))
 
         def gather2(c):
-            if c >= 2:
-                g2_s[c] = lay.tile([P, CHUNK], U8, name="g2_s%d" % c, align_bytes=64, offset=2048 * (c - 2) + 1024)[:]
-                g2_w[c] = lay.tile([P, CHUNK], U32, name="g2_w%d" % c, align_bytes=64, offset=2048 * (c - 2))[:]
-            else:
-                g2_s[c] = first_s[:, c * CHUNK : (c + 1) * CHUNK]
-                g2_w[c] = first_w[:, c * CHUNK : (c + 1) * CHUNK]
+            words_at, scales_at = ((8192, 9216), (12800, 13824), (8192, 9216), (0, 1024))[c]
+            g2_s[c] = lay.tile([P, CHUNK], U8, name="g2_s%d" % c, align_bytes=64, offset=scales_at)[:]
+            g2_w[c] = lay.tile([P, CHUNK], U32, name="g2_w%d" % c, align_bytes=64, offset=words_at)[:]
             nc.vector.tensor_copy(g2_s[c], tab2_s[:].bitcast(U8).indirect(entries(list2, c)))
             nc.vector.tensor_copy(g2_w[c], tab2_w[:].bitcast(U32).indirect(entries(list2, c)))
 
@@ -173,7 +173,7 @@ def tile_list_kg_relu_none_kernel(
         def deal_scales():
             nc.vector.tensor_copy(
                 w_s[:].rearrange("p (t m) -> p t m", t=PACK),
-                ws_raw[:].bitcast(U8).rearrange("p (m t) -> p t m", t=PACK),
+                ws_raw.bitcast(U8).rearrange("p (m t) -> p t m", t=PACK),
             )
 
         def gather1_scales():
@@ -183,21 +183,28 @@ def tile_list_kg_relu_none_kernel(
         deal_wb()
         gather1_scales()
         gather1(0)
-        gather1(1)
         deal_scales()
+        gather1(1)
+        g1_w[2] = mid_w[:, CHUNK : 2 * CHUNK]
+        g1_w[3] = mid_w[:, 2 * CHUNK : 3 * CHUNK]
+        nc.vector.tensor_copy(mid_w[:, CHUNK:], tab1_w[:].bitcast(U32).indirect(list1[:, J // 32 :]))
         last = chunks - 1
         for c in range(2):
             open_sum(c, 0)
             open_sum(c, 1)
-        for c in range(chunks):
+        for c in range(last):
             gather2(c)
-            if c > 0:
-                score(c - 1, 0, CHUNK, False, nc.sync)
-            close_sum(c, 0, c == last)
+            if c == 2:
+                score(0, 0, CHUNK, False, nc.sync)
+            close_sum(c, 0, False)
             close_sum(c, 1, False)
             if c + 2 < chunks:
-                gather1(c + 2)
                 open_sum(c + 2, 0)
                 open_sum(c + 2, 1)
+        gather2(last)
+        score(1, 0, CHUNK, False, nc.sync)
+        close_sum(last, 0, True)
+        close_sum(last, 1, False)
         score(last, 0, SUB, True, nc.sync)
-        score(last, SUB, SUB, False, nc.scalar)
+        score(2, 0, CHUNK, False, nc.scalar)
+        score(last, SUB, SUB, True, nc.sync)

@@ -37,8 +37,8 @@ def tile_list_kg_relu_none_kernel(
     with ExitStack() as ctx:
         keep = ctx.enter_context(tc.tile_pool(name="keep", bufs=1))
         lay = ctx.enter_context(tc.tile_pool(name="lay", bufs=1))
-        zps = ctx.enter_context(tc.psum_pool(name="zps", bufs=5))
-        yps = ctx.enter_context(tc.psum_pool(name="yps", bufs=3))
+        zps = ctx.enter_context(tc.psum_pool(name="zps", bufs=4))
+        yps = ctx.enter_context(tc.psum_pool(name="yps", bufs=4))
 
         list1 = keep.tile([P, J // 16], U16, name="list1")
         list2 = keep.tile([P, J // 16], U16, name="list2")
@@ -87,7 +87,7 @@ def tile_list_kg_relu_none_kernel(
         g2_s = {}
         z = {}
         w_s = lay.tile([P, R], U8, name="w_s", align_bytes=64, offset=14336)
-        mid_w = lay.tile([P, 3 * CHUNK], U32, name="mid_w", align_bytes=64, offset=9728)
+        mid_w = lay.tile([P, 3 * CHUNK], U32, name="mid_w", align_bytes=64, offset=14848)
         h = [lay.tile([P, CHUNK, PACK], BF16, name="h%d" % c, align_bytes=64, offset=2048 * c) for c in range(chunks)]
         h_w = [keep.tile([P, CHUNK], U32, name="h_w%d" % c, align_bytes=64) for c in range(chunks)]
         h_s = [keep.tile([P, CHUNK], U8, name="h_s%d" % c, align_bytes=64) for c in range(chunks)]
@@ -106,8 +106,8 @@ def tile_list_kg_relu_none_kernel(
             words_at, scales_at = ((8192, 9216), (12800, 13824), (8192, 9216), (0, 1024))[c]
             g2_s[c] = lay.tile([P, CHUNK], U8, name="g2_s%d" % c, align_bytes=64, offset=scales_at)[:]
             g2_w[c] = lay.tile([P, CHUNK], U32, name="g2_w%d" % c, align_bytes=64, offset=words_at)[:]
-            nc.vector.tensor_copy(g2_s[c], tab2_s[:].bitcast(U8).indirect(entries(list2, c)))
             nc.vector.tensor_copy(g2_w[c], tab2_w[:].bitcast(U32).indirect(entries(list2, c)))
+            nc.vector.tensor_copy(g2_s[c], tab2_s[:].bitcast(U8).indirect(entries(list2, c)))
 
         def open_sum(c, s):
             cols = slice(s * SUB, (s + 1) * SUB)
@@ -136,7 +136,7 @@ def tile_list_kg_relu_none_kernel(
             else:
                 nc.scalar.activation(out=h[c][:, cols, :], in_=src, func=RELU)
 
-        def score(c, lo, width, on_vector, queue):
+        def score(c, lo, width):
             cols = slice(lo, lo + width)
             nc.vector.quantize_mx(
                 out=h_w[c][:, cols].bitcast(E4M3), scales=h_s[c][:, cols],
@@ -150,6 +150,9 @@ def tile_list_kg_relu_none_kernel(
                     rhs=h_w[c][:, cols].bitcast(E4M3), rhs_scale=h_s[c][:, cols],
                     start=True, stop=True,
                 )
+            return y
+
+        def store(y, c, lo, width, on_vector, queue):
             res = keep.tile([P, 2, width], F32, name="res%d_%d" % (c, lo))
             if on_vector:
                 nc.vector.tensor_copy(res[:], y[:])
@@ -171,7 +174,7 @@ def tile_list_kg_relu_none_kernel(
             )
 
         def deal_scales():
-            nc.vector.tensor_copy(
+            nc.gpsimd.tensor_copy(
                 w_s[:].rearrange("p (t m) -> p t m", t=PACK),
                 ws_raw.bitcast(U8).rearrange("p (m t) -> p t m", t=PACK),
             )
@@ -195,16 +198,20 @@ def tile_list_kg_relu_none_kernel(
         for c in range(last):
             gather2(c)
             if c == 2:
-                score(0, 0, CHUNK, False, nc.sync)
+                store(score(0, 0, CHUNK), 0, 0, CHUNK, False, nc.sync)
             close_sum(c, 0, False)
             close_sum(c, 1, False)
             if c + 2 < chunks:
                 open_sum(c + 2, 0)
                 open_sum(c + 2, 1)
         gather2(last)
-        score(1, 0, CHUNK, False, nc.sync)
+        y1 = score(1, 0, CHUNK)
         close_sum(last, 0, True)
         close_sum(last, 1, False)
-        score(last, 0, SUB, True, nc.sync)
-        score(2, 0, CHUNK, False, nc.scalar)
-        score(last, SUB, SUB, True, nc.sync)
+        y2 = score(2, 0, CHUNK)
+        y3 = score(last, 0, SUB)
+        store(y1, 1, 0, CHUNK, True, nc.sync)
+        store(y2, 2, 0, CHUNK, False, nc.scalar)
+        y4 = score(last, SUB, SUB)
+        store(y3, last, 0, SUB, True, nc.sync)
+        store(y4, last, SUB, SUB, True, nc.sync)

@@ -40,74 +40,68 @@ def tile_list_kg_relu_none_kernel(
         zps = ctx.enter_context(tc.psum_pool(name="zps", bufs=4))
         yps = ctx.enter_context(tc.psum_pool(name="yps", bufs=4))
 
+        A = 2048
+        B = 6144
+        H0 = 10240
         list1 = keep.tile([P, J // 16], U16, name="list1")
         list2 = keep.tile([P, J // 16], U16, name="list2")
         tab1_w = keep.tile([P, T], I32, name="tab1_w", align_bytes=64)
         tab2_w = keep.tile([P, T], I32, name="tab2_w", align_bytes=64)
-        tab1_s = lay.tile([P, T // 4], I32, name="tab1_s", align_bytes=64, offset=13312)
-        tab2_s = keep.tile([P, T // 4], I32, name="tab2_s", align_bytes=64)
-        wa_raw = keep.tile([P, R // 2], I32, name="wa_raw", align_bytes=64)
-        wb_raw = keep.tile([P, R], I32, name="wb_raw", tag="early", align_bytes=64)
-        ws_tile = lay.tile([P, 160], I32, name="ws_tile", align_bytes=64, offset=9152)
-        ws_raw = ws_tile[:, 0 : R // 4]
+        tab1_s = lay.tile([P, T // 4], I32, name="tab1_s", align_bytes=64, offset=A)
+        tab2_s = lay.tile([P, T // 4], I32, name="tab2_s", align_bytes=64, offset=B)
+        wa_raw = keep.tile([P, R // 2], I32, name="wa_raw", tag="early", align_bytes=64)
+        wb_raw = keep.tile([P, R], I32, name="wb_raw", align_bytes=64)
+        was_raw = keep.tile([P, R // 4], I32, name="was_raw", align_bytes=64)
+        wbs_raw = keep.tile([P, R // 4], I32, name="wbs_raw", align_bytes=64)
         wa_w = keep.tile([P, R], U16, name="wa_w", align_bytes=64)
         wb_w = keep.tile([P, R], I32, name="wb_w", align_bytes=64)
+        wa_s = keep.tile([P, R], U8, name="wa_s", align_bytes=64)
+        wb_s = keep.tile([P, R], U8, name="wb_s", align_bytes=64)
         en_w = keep.tile([P, N // 2], I32, name="en_w", align_bytes=64)
         en_s = keep.tile([P, N // 4], I32, name="en_s", align_bytes=64)
-        tab1_src = tab_words[0].rearrange("p t i -> p (t i)").bitcast(I32)
-        tab2_src = tab2_words[0].rearrange("p t i -> p (t i)").bitcast(I32)
-        wb_src = wb_words[0].rearrange("p r i -> p (r i)").bitcast(I32)
-        both = (nc.sync, nc.scalar)
-
         warm = keep.tile([P, 8], F32, name="warm")
         warm_out = keep.tile([P, 8], F32, name="warm_out")
+        both = (nc.sync, nc.scalar)
+
         nc.vector.memset(tab1_s[:], 0)
-        nc.vector.memset(ws_raw, 0)
+        nc.vector.memset(was_raw[:], 0)
         nc.vector.memset(tab2_s[:], 0)
+        nc.vector.memset(wbs_raw[:], 0)
 
         nc.scalar.dma_start(out=wa_raw[:], in_=wa_words[0].bitcast(I32))
-        nc.scalar.dma_start(out=wb_raw[:], in_=wb_src)
+        nc.scalar.dma_start(out=wb_raw[:], in_=wb_words[0].rearrange("p r i -> p (r i)").bitcast(I32))
         nc.sync.dma_start(list1[:], offs)
-        nc.gpsimd.dma_start(out=tab1_w[:], in_=tab1_src)
+        nc.gpsimd.dma_start(out=tab1_w[:], in_=tab_words[0].rearrange("p t i -> p (t i)").bitcast(I32))
         nc.gpsimd.dma_start(out=en_w[:], in_=en_words[0].bitcast(I32))
         nc.gpsimd.memset(en_s[:], 0)
         nc.gpsimd.memset(warm[:], 0.0)
-        nc.gpsimd.dma_start(out=tab2_w[:], in_=tab2_src)
+        nc.gpsimd.dma_start(out=tab2_w[:], in_=tab2_words[0].rearrange("p t i -> p (t i)").bitcast(I32))
         load_scales(both, tab1_s[:], 0, tab_scales)
         nc.sync.dma_start(list2[:], offs2)
-        load_scales(both, ws_raw, 0, wa_scales)
-        load_scales(both, ws_raw, ROW2, wb_scales)
+        load_scales(both, was_raw[:], 0, wa_scales)
         load_scales(both, tab2_s[:], ROW2, tab2_scales)
+        load_scales(both, wbs_raw[:], ROW2, wb_scales)
         nc.scalar.activation(out=warm_out[:], in_=warm[:], func=RELU)
         load_scales((nc.sync,), en_s[:], 0, en_scales)
 
         g1_s = keep.tile([P, J], U8, name="g1_s", tag="early", align_bytes=64)
         g1_w = {}
         g2_w = {}
-        g2_s = {}
         z = {}
-        w_s = lay.tile([P, R], U8, name="w_s", align_bytes=64, offset=14336)
-        mid_w = lay.tile([P, 3 * CHUNK], U32, name="mid_w", align_bytes=64, offset=14848)
-        h = [lay.tile([P, CHUNK, PACK], BF16, name="h%d" % c, align_bytes=64, offset=2048 * c) for c in range(chunks)]
+        h = [lay.tile([P, CHUNK, PACK], BF16, name="h%d" % c, align_bytes=64, offset=H0 + 4096 * c) for c in range(chunks)]
         h_w = [keep.tile([P, CHUNK], U32, name="h_w%d" % c, align_bytes=64) for c in range(chunks)]
         h_s = [keep.tile([P, CHUNK], U8, name="h_s%d" % c, align_bytes=64) for c in range(chunks)]
 
-        def entries(lst, c):
-            return lst[:, c * (CHUNK // 16) : (c + 1) * (CHUNK // 16)]
+        def gather(name, dtype, at, window, lst, lo, width):
+            got = lay.tile([P, width], dtype, name=name, align_bytes=64, offset=at)
+            nc.vector.tensor_copy(got[:], window[:].bitcast(dtype).indirect(lst[:, lo // 16 : (lo + width) // 16]))
+            return got
 
-        def gather1(c):
-            if c > 0:
-                g1_w[c] = mid_w[:, (c - 1) * CHUNK : c * CHUNK]
-            else:
-                g1_w[c] = lay.tile([P, CHUNK], U32, name="g1_w%d" % c, align_bytes=64, offset=13312)[:]
-            nc.vector.tensor_copy(g1_w[c], tab1_w[:].bitcast(U32).indirect(entries(list1, c)))
-
-        def gather2(c):
-            words_at, scales_at = ((8192, 9216), (12800, 13824), (8192, 9216), (0, 1024))[c]
-            g2_s[c] = lay.tile([P, CHUNK], U8, name="g2_s%d" % c, align_bytes=64, offset=scales_at)[:]
-            g2_w[c] = lay.tile([P, CHUNK], U32, name="g2_w%d" % c, align_bytes=64, offset=words_at)[:]
-            nc.vector.tensor_copy(g2_w[c], tab2_w[:].bitcast(U32).indirect(entries(list2, c)))
-            nc.vector.tensor_copy(g2_s[c], tab2_s[:].bitcast(U8).indirect(entries(list2, c)))
+        def deal_scales(dealt, raw):
+            nc.gpsimd.tensor_copy(
+                dealt[:].rearrange("p (t m) -> p t m", t=PACK),
+                raw[:].bitcast(U8).rearrange("p (m t) -> p t m", t=PACK),
+            )
 
         def open_sum(c, s):
             cols = slice(s * SUB, (s + 1) * SUB)
@@ -116,18 +110,19 @@ def tile_list_kg_relu_none_kernel(
             for t in range(PACK):
                 rows = slice(t * P, (t + 1) * P)
                 nc.tensor.matmul_mx(
-                    out=z[c, s][:, t, :], lhsT=wa_w[:, rows].bitcast(E2M1), lhsT_scale=w_s[:, rows],
+                    out=z[c, s][:, t, :], lhsT=wa_w[:, rows].bitcast(E2M1), lhsT_scale=wa_s[:, rows],
                     rhs=g1_w[c][:, cols].bitcast(E4M3), rhs_scale=g1_s[:, j0 : j0 + SUB],
                     start=(t == 0), stop=False,
                 )
 
         def close_sum(c, s, on_vector):
             cols = slice(s * SUB, (s + 1) * SUB)
+            j0 = c * CHUNK + s * SUB
             for t in range(PACK):
                 rows = slice(t * P, (t + 1) * P)
                 nc.tensor.matmul_mx(
-                    out=z[c, s][:, t, :], lhsT=wb_w[:, rows].bitcast(E4M3), lhsT_scale=w_s[ROW2:P, rows],
-                    rhs=g2_w[c][:, cols].bitcast(E4M3), rhs_scale=g2_s[c][ROW2:P, cols],
+                    out=z[c, s][:, t, :], lhsT=wb_w[:, rows].bitcast(E4M3), lhsT_scale=wb_s[ROW2:P, rows],
+                    rhs=g2_w[c][:, cols].bitcast(E4M3), rhs_scale=g2_s[ROW2:P, j0 : j0 + SUB],
                     start=False, stop=(t == PACK - 1),
                 )
             src = z[c, s][:].rearrange("p t j -> p j t")
@@ -168,50 +163,46 @@ def tile_list_kg_relu_none_kernel(
             )
 
         def deal_wb():
-            nc.vector.tensor_copy(
-                wb_w[:].rearrange("p (t m) -> p m t", t=PACK),
-                wb_raw[:].rearrange("p (m t) -> p m t", t=PACK),
-            )
-
-        def deal_scales():
             nc.gpsimd.tensor_copy(
-                w_s[:].rearrange("p (t m) -> p t m", t=PACK),
-                ws_raw.bitcast(U8).rearrange("p (m t) -> p t m", t=PACK),
+                wb_w[:].rearrange("p (t m) -> p t m", t=PACK),
+                wb_raw[:].rearrange("p (m t) -> p t m", t=PACK),
             )
-
-        def gather1_scales():
-            nc.vector.tensor_copy(g1_s[:], tab1_s[:].bitcast(U8).indirect(list1[:]))
 
         deal_wa()
         deal_wb()
-        gather1_scales()
-        gather1(0)
-        deal_scales()
-        gather1(1)
-        g1_w[2] = mid_w[:, CHUNK : 2 * CHUNK]
-        g1_w[3] = mid_w[:, 2 * CHUNK : 3 * CHUNK]
-        nc.vector.tensor_copy(mid_w[:, CHUNK:], tab1_w[:].bitcast(U32).indirect(list1[:, J // 32 :]))
-        last = chunks - 1
+        nc.vector.tensor_copy(g1_s[:], tab1_s[:].bitcast(U8).indirect(list1[:]))
+        deal_scales(wa_s, was_raw)
+        deal_scales(wb_s, wbs_raw)
+        g1_w[0] = gather("g1_w0", U32, A - 768, tab1_w, list1, 0, CHUNK)
+        g1_w[1] = gather("g1_w1", U32, A + 256, tab1_w, list1, CHUNK, CHUNK)
+        g2_s = gather("g2_s", U8, A + 1280, tab2_s, list2, 0, J)
         for c in range(2):
             open_sum(c, 0)
             open_sum(c, 1)
-        for c in range(last):
-            gather2(c)
-            if c == 2:
-                store(score(0, 0, CHUNK), 0, 0, CHUNK, False, nc.sync)
+        g2_w[0] = gather("g2_w0", U32, B - 512, tab2_w, list2, 0, CHUNK)
+        g2_w[1] = gather("g2_w1", U32, B + 1024, tab2_w, list2, CHUNK, CHUNK)
+        for c in range(2):
             close_sum(c, 0, False)
             close_sum(c, 1, False)
-            if c + 2 < chunks:
-                open_sum(c + 2, 0)
-                open_sum(c + 2, 1)
-        gather2(last)
+        g1_w[2] = gather("g1_w2", U32, B - 1024, tab1_w, list1, 2 * CHUNK, CHUNK)
+        g2_w[2] = gather("g2_w2", U32, B, tab2_w, list2, 2 * CHUNK, CHUNK)
+        open_sum(2, 0)
+        open_sum(2, 1)
+        close_sum(2, 0, False)
+        close_sum(2, 1, False)
+        y0 = score(0, 0, CHUNK)
+        g1_w[3] = gather("g1_w3", U32, H0, tab1_w, list1, 3 * CHUNK, CHUNK)
+        g2_w[3] = gather("g2_w3", U32, H0 + 1024, tab2_w, list2, 3 * CHUNK, CHUNK)
+        store(y0, 0, 0, CHUNK, False, nc.sync)
+        open_sum(3, 0)
+        open_sum(3, 1)
         y1 = score(1, 0, CHUNK)
-        close_sum(last, 0, True)
-        close_sum(last, 1, False)
+        close_sum(3, 0, True)
+        close_sum(3, 1, False)
         y2 = score(2, 0, CHUNK)
-        y3 = score(last, 0, SUB)
-        store(y1, 1, 0, CHUNK, True, nc.sync)
+        y3 = score(3, 0, SUB)
+        y4 = score(3, SUB, SUB)
+        store(y1, 1, 0, CHUNK, False, nc.sync)
         store(y2, 2, 0, CHUNK, False, nc.scalar)
-        y4 = score(last, SUB, SUB)
-        store(y3, last, 0, SUB, True, nc.sync)
-        store(y4, last, SUB, SUB, True, nc.sync)
+        store(y3, 3, 0, SUB, True, nc.sync)
+        store(y4, 3, SUB, SUB, True, nc.sync)

@@ -69,13 +69,13 @@ def tile_list_kg_relu_none_kernel(
         nc.vector.memset(wbs_raw[:], 0)
 
         nc.scalar.dma_start(out=wa_raw[:], in_=wa_words[0].bitcast(I32))
-        nc.scalar.dma_start(out=wb_raw[:], in_=wb_words[0].rearrange("p r i -> p (r i)").bitcast(I32))
         nc.sync.dma_start(list1[:], offs)
         nc.gpsimd.dma_start(out=tab1_w[:], in_=tab_words[0].rearrange("p t i -> p (t i)").bitcast(I32))
-        nc.gpsimd.dma_start(out=en_w[:], in_=en_words[0].bitcast(I32))
+        nc.gpsimd.dma_start(out=wb_raw[:], in_=wb_words[0].rearrange("p r i -> p (r i)").bitcast(I32))
         nc.gpsimd.memset(en_s[:], 0)
         nc.gpsimd.memset(warm[:], 0.0)
         nc.gpsimd.dma_start(out=tab2_w[:], in_=tab2_words[0].rearrange("p t i -> p (t i)").bitcast(I32))
+        nc.gpsimd.dma_start(out=en_w[:], in_=en_words[0].bitcast(I32))
         load_scales(both, tab1_s[:], 0, tab_scales)
         nc.sync.dma_start(list2[:], offs2)
         load_scales(both, was_raw[:], 0, wa_scales)
@@ -169,12 +169,13 @@ def tile_list_kg_relu_none_kernel(
             )
 
         deal_wa()
-        deal_wb()
         nc.vector.tensor_copy(g1_s[:], tab1_s[:].bitcast(U8).indirect(list1[:]))
         deal_scales(wa_s, was_raw)
+        deal_wb()
         deal_scales(wb_s, wbs_raw)
-        g1_w[0] = gather("g1_w0", U32, A - 768, tab1_w, list1, 0, CHUNK)
-        g1_w[1] = gather("g1_w1", U32, A + 256, tab1_w, list1, CHUNK, CHUNK)
+        first = gather("g1_first", U32, A - 768, tab1_w, list1, 0, 2 * CHUNK)
+        g1_w[0] = first[:, 0:CHUNK]
+        g1_w[1] = first[:, CHUNK:]
         g2_s = gather("g2_s", U8, A + 1280, tab2_s, list2, 0, J)
         for c in range(2):
             open_sum(c, 0)
@@ -203,6 +204,6 @@ def tile_list_kg_relu_none_kernel(
         y3 = score(3, 0, SUB)
         y4 = score(3, SUB, SUB)
         store(y1, 1, 0, CHUNK, False, nc.sync)
-        store(y2, 2, 0, CHUNK, False, nc.scalar)
-        store(y3, 3, 0, SUB, True, nc.sync)
+        store(y2, 2, 0, CHUNK, False, nc.sync)
+        store(y3, 3, 0, SUB, False, nc.scalar)
         store(y4, 3, SUB, SUB, True, nc.sync)

@@ -59,8 +59,6 @@ def tile_list_kg_relu_none_kernel(
         wb_s = keep.tile([P, R], U8, name="wb_s", align_bytes=64)
         en_w = keep.tile([P, N // 2], I32, name="en_w", align_bytes=64)
         en_s = keep.tile([P, N // 4], I32, name="en_s", align_bytes=64)
-        warm = keep.tile([P, 8], F32, name="warm")
-        warm_out = keep.tile([P, 8], F32, name="warm_out")
         both = (nc.sync, nc.scalar)
 
         nc.vector.memset(tab1_s[:], 0)
@@ -73,7 +71,6 @@ def tile_list_kg_relu_none_kernel(
         nc.gpsimd.dma_start(out=tab1_w[:], in_=tab_words[0].rearrange("p t i -> p (t i)").bitcast(I32))
         nc.gpsimd.dma_start(out=wb_raw[:], in_=wb_words[0].rearrange("p r i -> p (r i)").bitcast(I32))
         nc.gpsimd.memset(en_s[:], 0)
-        nc.gpsimd.memset(warm[:], 0.0)
         nc.gpsimd.dma_start(out=tab2_w[:], in_=tab2_words[0].rearrange("p t i -> p (t i)").bitcast(I32))
         nc.gpsimd.dma_start(out=en_w[:], in_=en_words[0].bitcast(I32))
         load_scales(both, tab1_s[:], 0, tab_scales)
@@ -81,7 +78,6 @@ def tile_list_kg_relu_none_kernel(
         load_scales(both, was_raw[:], 0, wa_scales)
         load_scales(both, tab2_s[:], ROW2, tab2_scales)
         load_scales(both, wbs_raw[:], ROW2, wb_scales)
-        nc.scalar.activation(out=warm_out[:], in_=warm[:], func=RELU)
         load_scales((nc.sync,), en_s[:], 0, en_scales)
 
         g1_s = keep.tile([P, J], U8, name="g1_s", tag="early", align_bytes=64)

@@ -37,12 +37,12 @@ def tile_list_kg_relu_none_kernel(
     with ExitStack() as ctx:
         keep = ctx.enter_context(tc.tile_pool(name="keep", bufs=1))
         lay = ctx.enter_context(tc.tile_pool(name="lay", bufs=1))
-        zps = ctx.enter_context(tc.psum_pool(name="zps", bufs=4))
-        yps = ctx.enter_context(tc.psum_pool(name="yps", bufs=4))
+        banks = ctx.enter_context(tc.psum_pool(name="banks", bufs=1))
 
-        A = 2048
-        B = 6144
+        A = 4096
+        B = 8192
         H0 = 10240
+        W = 1024
         list1 = keep.tile([P, J // 16], U16, name="list1")
         list2 = keep.tile([P, J // 16], U16, name="list2")
         tab1_w = keep.tile([P, T], I32, name="tab1_w", align_bytes=64)
@@ -52,7 +52,7 @@ def tile_list_kg_relu_none_kernel(
         wa_raw = keep.tile([P, R // 2], I32, name="wa_raw", tag="early", align_bytes=64)
         wb_raw = keep.tile([P, R], I32, name="wb_raw", align_bytes=64)
         was_raw = keep.tile([P, R // 4], I32, name="was_raw", align_bytes=64)
-        wbs_raw = keep.tile([P, R // 4], I32, name="wbs_raw", align_bytes=64)
+        wbs_raw = lay.tile([P, R // 4], I32, name="wbs_raw", align_bytes=64, offset=W)
         wa_w = keep.tile([P, R], U16, name="wa_w", align_bytes=64)
         wb_w = keep.tile([P, R], I32, name="wb_w", align_bytes=64)
         wa_s = keep.tile([P, R], U8, name="wa_s", align_bytes=64)
@@ -83,6 +83,7 @@ def tile_list_kg_relu_none_kernel(
         g1_s = keep.tile([P, J], U8, name="g1_s", tag="early", align_bytes=64)
         g1_w = {}
         g2_w = {}
+        g2_s = {}
         z = {}
         h = [lay.tile([P, CHUNK, PACK], BF16, name="h%d" % c, align_bytes=64, offset=H0 + 4096 * c) for c in range(chunks)]
         h_w = [keep.tile([P, CHUNK], U32, name="h_w%d" % c, align_bytes=64) for c in range(chunks)]
@@ -102,7 +103,7 @@ def tile_list_kg_relu_none_kernel(
         def open_sum(c, s):
             cols = slice(s * SUB, (s + 1) * SUB)
             j0 = c * CHUNK + s * SUB
-            z[c, s] = zps.tile([P, PACK, SUB], F32, name="z")
+            z[c, s] = banks.tile([P, PACK, SUB], F32, name="z%d_%d" % (c, s), tag="bank%d" % (2 * (c % 3) + s))
             for t in range(PACK):
                 rows = slice(t * P, (t + 1) * P)
                 nc.tensor.matmul_mx(
@@ -113,12 +114,12 @@ def tile_list_kg_relu_none_kernel(
 
         def close_sum(c, s, on_vector):
             cols = slice(s * SUB, (s + 1) * SUB)
-            j0 = c * CHUNK + s * SUB
+            j0 = (c % 2) * CHUNK + s * SUB
             for t in range(PACK):
                 rows = slice(t * P, (t + 1) * P)
                 nc.tensor.matmul_mx(
                     out=z[c, s][:, t, :], lhsT=wb_w[:, rows].bitcast(E4M3), lhsT_scale=wb_s[ROW2:P, rows],
-                    rhs=g2_w[c][:, cols].bitcast(E4M3), rhs_scale=g2_s[ROW2:P, j0 : j0 + SUB],
+                    rhs=g2_w[c][:, cols].bitcast(E4M3), rhs_scale=g2_s[c // 2][ROW2:P, j0 : j0 + SUB],
                     start=False, stop=(t == PACK - 1),
                 )
             src = z[c, s][:].rearrange("p t j -> p j t")
@@ -127,13 +128,13 @@ def tile_list_kg_relu_none_kernel(
             else:
                 nc.scalar.activation(out=h[c][:, cols, :], in_=src, func=RELU)
 
-        def score(c, lo, width):
+        def score(c, lo, width, bank):
             cols = slice(lo, lo + width)
             nc.vector.quantize_mx(
                 out=h_w[c][:, cols].bitcast(E4M3), scales=h_s[c][:, cols],
                 in_=h[c][:, cols, :].rearrange("p j t -> p (j t)"),
             )
-            y = yps.tile([P, 2, width], F32, name="y")
+            y = banks.tile([P, 2, width], F32, name="y%d_%d" % (c, lo), tag="bank%d" % bank)
             for u in range(2):
                 nc.tensor.matmul_mx(
                     out=y[:, u, :], lhsT=en_w[:, u * 64 : (u + 1) * 64].bitcast(E2M1),
@@ -169,36 +170,37 @@ def tile_list_kg_relu_none_kernel(
         deal_scales(wa_s, was_raw)
         deal_wb()
         deal_scales(wb_s, wbs_raw)
-        first = gather("g1_first", U32, A - 768, tab1_w, list1, 0, 2 * CHUNK)
+        first = gather("g1_first", U32, A - 1536, tab1_w, list1, 0, 2 * CHUNK)
         g1_w[0] = first[:, 0:CHUNK]
         g1_w[1] = first[:, CHUNK:]
-        g2_s = gather("g2_s", U8, A + 1280, tab2_s, list2, 0, J)
+        g2_s[0] = gather("g2_s0", U8, A + 1536, tab2_s, list2, 0, J // 2)
         for c in range(2):
             open_sum(c, 0)
             open_sum(c, 1)
-        g2_w[0] = gather("g2_w0", U32, B - 512, tab2_w, list2, 0, CHUNK)
-        g2_w[1] = gather("g2_w1", U32, B + 1024, tab2_w, list2, CHUNK, CHUNK)
+        g2_w[0] = gather("g2_w0", U32, B - 2048, tab2_w, list2, 0, CHUNK)
+        g2_w[1] = gather("g2_w1", U32, B - 1024, tab2_w, list2, CHUNK, CHUNK)
         for c in range(2):
             close_sum(c, 0, False)
             close_sum(c, 1, False)
-        g1_w[2] = gather("g1_w2", U32, B - 1024, tab1_w, list1, 2 * CHUNK, CHUNK)
-        g2_w[2] = gather("g2_w2", U32, B, tab2_w, list2, 2 * CHUNK, CHUNK)
+        g2_s[1] = gather("g2_s1", U8, A - 1024, tab2_s, list2, J // 2, J // 2)
+        g1_w[2] = gather("g1_w2", U32, W - 768, tab1_w, list1, 2 * CHUNK, CHUNK)
+        g2_w[2] = gather("g2_w2", U32, W + 256, tab2_w, list2, 2 * CHUNK, CHUNK)
         open_sum(2, 0)
         open_sum(2, 1)
         close_sum(2, 0, False)
         close_sum(2, 1, False)
-        y0 = score(0, 0, CHUNK)
+        y0 = score(0, 0, CHUNK, 6)
         g1_w[3] = gather("g1_w3", U32, H0, tab1_w, list1, 3 * CHUNK, CHUNK)
         g2_w[3] = gather("g2_w3", U32, H0 + 1024, tab2_w, list2, 3 * CHUNK, CHUNK)
         store(y0, 0, 0, CHUNK, False, nc.sync)
         open_sum(3, 0)
         open_sum(3, 1)
-        y1 = score(1, 0, CHUNK)
+        y1 = score(1, 0, CHUNK, 7)
         close_sum(3, 0, True)
         close_sum(3, 1, False)
-        y2 = score(2, 0, CHUNK)
-        y3 = score(3, 0, SUB)
-        y4 = score(3, SUB, SUB)
+        y2 = score(2, 0, CHUNK, 2)
+        y3 = score(3, 0, SUB, 3)
+        y4 = score(3, SUB, SUB, 4)
         store(y1, 1, 0, CHUNK, False, nc.sync)
         store(y2, 2, 0, CHUNK, False, nc.sync)
         store(y3, 3, 0, SUB, False, nc.scalar)

@@ -42,7 +42,6 @@ def tile_list_kg_relu_none_kernel(
         A = 4096
         B = 8192
         H0 = 10240
-        W = 1024
         list1 = keep.tile([P, J // 16], U16, name="list1")
         list2 = keep.tile([P, J // 16], U16, name="list2")
         tab1_w = keep.tile([P, T], I32, name="tab1_w", align_bytes=64)
@@ -52,7 +51,7 @@ def tile_list_kg_relu_none_kernel(
         wa_raw = keep.tile([P, R // 2], I32, name="wa_raw", tag="early", align_bytes=64)
         wb_raw = keep.tile([P, R], I32, name="wb_raw", align_bytes=64)
         was_raw = keep.tile([P, R // 4], I32, name="was_raw", align_bytes=64)
-        wbs_raw = lay.tile([P, R // 4], I32, name="wbs_raw", align_bytes=64, offset=W)
+        wbs_raw = keep.tile([P, R // 4], I32, name="wbs_raw", align_bytes=64)
         wa_w = keep.tile([P, R], U16, name="wa_w", align_bytes=64)
         wb_w = keep.tile([P, R], I32, name="wb_w", align_bytes=64)
         wa_s = keep.tile([P, R], U8, name="wa_s", align_bytes=64)
@@ -103,7 +102,7 @@ def tile_list_kg_relu_none_kernel(
         def open_sum(c, s):
             cols = slice(s * SUB, (s + 1) * SUB)
             j0 = c * CHUNK + s * SUB
-            z[c, s] = banks.tile([P, PACK, SUB], F32, name="z%d_%d" % (c, s), tag="bank%d" % (2 * (c % 3) + s))
+            z[c, s] = banks.tile([P, PACK, SUB], F32, name="z%d_%d" % (c, s), tag="bank%d" % (2 * (0, 1, 0, 2)[c] + s))
             for t in range(PACK):
                 rows = slice(t * P, (t + 1) * P)
                 nc.tensor.matmul_mx(
@@ -173,6 +172,7 @@ def tile_list_kg_relu_none_kernel(
         first = gather("g1_first", U32, A - 1536, tab1_w, list1, 0, 2 * CHUNK)
         g1_w[0] = first[:, 0:CHUNK]
         g1_w[1] = first[:, CHUNK:]
+        g1_w[2] = gather("g1_w2", U32, A + 512, tab1_w, list1, 2 * CHUNK, CHUNK)
         g2_s[0] = gather("g2_s0", U8, A + 1536, tab2_s, list2, 0, J // 2)
         for c in range(2):
             open_sum(c, 0)
@@ -182,9 +182,8 @@ def tile_list_kg_relu_none_kernel(
         for c in range(2):
             close_sum(c, 0, False)
             close_sum(c, 1, False)
+        g2_w[2] = gather("g2_w2", U32, 1024, tab2_w, list2, 2 * CHUNK, CHUNK)
         g2_s[1] = gather("g2_s1", U8, A - 1024, tab2_s, list2, J // 2, J // 2)
-        g1_w[2] = gather("g1_w2", U32, W - 768, tab1_w, list1, 2 * CHUNK, CHUNK)
-        g2_w[2] = gather("g2_w2", U32, W + 256, tab2_w, list2, 2 * CHUNK, CHUNK)
         open_sum(2, 0)
         open_sum(2, 1)
         close_sum(2, 0, False)
@@ -200,7 +199,7 @@ def tile_list_kg_relu_none_kernel(
         close_sum(3, 1, False)
         y2 = score(2, 0, CHUNK, 2)
         y3 = score(3, 0, SUB, 3)
-        y4 = score(3, SUB, SUB, 4)
+        y4 = score(3, SUB, SUB, 0)
         store(y1, 1, 0, CHUNK, False, nc.sync)
         store(y2, 2, 0, CHUNK, False, nc.sync)
         store(y3, 3, 0, SUB, False, nc.scalar)

@@ -84,7 +84,7 @@ def tile_list_kg_relu_none_kernel(
         g2_w = {}
         g2_s = {}
         z = {}
-        h = [lay.tile([P, CHUNK, PACK], BF16, name="h%d" % c, align_bytes=64, offset=H0 + 4096 * c) for c in range(chunks)]
+        h = [lay.tile([P, CHUNK, PACK], BF16, name="h%d" % c, align_bytes=64, offset=H0 + 4096 * c) for c in range(chunks - 1)]
         h_w = [keep.tile([P, CHUNK], U32, name="h_w%d" % c, align_bytes=64) for c in range(chunks)]
         h_s = [keep.tile([P, CHUNK], U8, name="h_s%d" % c, align_bytes=64) for c in range(chunks)]
 
@@ -99,28 +99,34 @@ def tile_list_kg_relu_none_kernel(
                 raw[:].bitcast(U8).rearrange("p (m t) -> p t m", t=PACK),
             )
 
-        def open_sum(c, s):
+        def passes(c, s, table, first):
             cols = slice(s * SUB, (s + 1) * SUB)
-            j0 = c * CHUNK + s * SUB
-            z[c, s] = banks.tile([P, PACK, SUB], F32, name="z%d_%d" % (c, s), tag="bank%d" % (2 * (0, 1, 0, 2)[c] + s))
             for t in range(PACK):
                 rows = slice(t * P, (t + 1) * P)
-                nc.tensor.matmul_mx(
-                    out=z[c, s][:, t, :], lhsT=wa_w[:, rows].bitcast(E2M1), lhsT_scale=wa_s[:, rows],
-                    rhs=g1_w[c][:, cols].bitcast(E4M3), rhs_scale=g1_s[:, j0 : j0 + SUB],
-                    start=(t == 0), stop=False,
-                )
+                start = first and t == 0
+                stop = (not first) and t == PACK - 1
+                if table == 1:
+                    j0 = c * CHUNK + s * SUB
+                    nc.tensor.matmul_mx(
+                        out=z[c, s][:, t, :], lhsT=wa_w[:, rows].bitcast(E2M1), lhsT_scale=wa_s[:, rows],
+                        rhs=g1_w[c][:, cols].bitcast(E4M3), rhs_scale=g1_s[:, j0 : j0 + SUB],
+                        start=start, stop=stop,
+                    )
+                else:
+                    j0 = (c % 2) * CHUNK + s * SUB
+                    nc.tensor.matmul_mx(
+                        out=z[c, s][:, t, :], lhsT=wb_w[:, rows].bitcast(E4M3), lhsT_scale=wb_s[ROW2:P, rows],
+                        rhs=g2_w[c][:, cols].bitcast(E4M3), rhs_scale=g2_s[c // 2][ROW2:P, j0 : j0 + SUB],
+                        start=start, stop=stop,
+                    )
+
+        def open_sum(c, s):
+            z[c, s] = banks.tile([P, PACK, SUB], F32, name="z%d_%d" % (c, s), tag="bank%d" % (2 * (c % 2) + s))
+            passes(c, s, 2 if c == 3 else 1, True)
 
         def close_sum(c, s, on_vector):
             cols = slice(s * SUB, (s + 1) * SUB)
-            j0 = (c % 2) * CHUNK + s * SUB
-            for t in range(PACK):
-                rows = slice(t * P, (t + 1) * P)
-                nc.tensor.matmul_mx(
-                    out=z[c, s][:, t, :], lhsT=wb_w[:, rows].bitcast(E4M3), lhsT_scale=wb_s[ROW2:P, rows],
-                    rhs=g2_w[c][:, cols].bitcast(E4M3), rhs_scale=g2_s[c // 2][ROW2:P, j0 : j0 + SUB],
-                    start=False, stop=(t == PACK - 1),
-                )
+            passes(c, s, 1 if c == 3 else 2, False)
             src = z[c, s][:].rearrange("p t j -> p j t")
             if on_vector:
                 nc.vector.tensor_scalar_max(h[c][:, cols, :], src, 0.0)
@@ -184,21 +190,22 @@ def tile_list_kg_relu_none_kernel(
             close_sum(c, 1, False)
         g2_w[2] = gather("g2_w2", U32, 1024, tab2_w, list2, 2 * CHUNK, CHUNK)
         g2_s[1] = gather("g2_s1", U8, A - 1024, tab2_s, list2, J // 2, J // 2)
+        g2_w[3] = gather("g2_w3", U32, A - 2048, tab2_w, list2, 3 * CHUNK, CHUNK)
         open_sum(2, 0)
         open_sum(2, 1)
         close_sum(2, 0, False)
         close_sum(2, 1, False)
-        y0 = score(0, 0, CHUNK, 6)
-        g1_w[3] = gather("g1_w3", U32, H0, tab1_w, list1, 3 * CHUNK, CHUNK)
-        g2_w[3] = gather("g2_w3", U32, H0 + 1024, tab2_w, list2, 3 * CHUNK, CHUNK)
+        y0 = score(0, 0, CHUNK, 4)
+        y1 = score(1, 0, CHUNK, 5)
+        g1_w[3] = gather("g1_w3", U32, H0 + 4096, tab1_w, list1, 3 * CHUNK, CHUNK)
         store(y0, 0, 0, CHUNK, False, nc.sync)
         open_sum(3, 0)
         open_sum(3, 1)
-        y1 = score(1, 0, CHUNK, 7)
+        h.append(lay.tile([P, CHUNK, PACK], BF16, name="h3", align_bytes=64, offset=H0 + 4096 * 3))
         close_sum(3, 0, True)
         close_sum(3, 1, False)
-        y2 = score(2, 0, CHUNK, 2)
-        y3 = score(3, 0, SUB, 3)
+        y2 = score(2, 0, CHUNK, 6)
+        y3 = score(3, 0, SUB, 7)
         y4 = score(3, SUB, SUB, 0)
         store(y1, 1, 0, CHUNK, False, nc.sync)
         store(y2, 2, 0, CHUNK, False, nc.sync)

@@ -40,8 +40,8 @@ def tile_list_kg_relu_none_kernel(
         banks = ctx.enter_context(tc.psum_pool(name="banks", bufs=1))
 
         A = 4096
-        B = 8192
-        H0 = 10240
+        B = 9216
+        H0 = 11264
         list1 = keep.tile([P, J // 16], U16, name="list1")
         list2 = keep.tile([P, J // 16], U16, name="list2")
         tab1_w = keep.tile([P, T], I32, name="tab1_w", align_bytes=64)
@@ -84,7 +84,8 @@ def tile_list_kg_relu_none_kernel(
         g2_w = {}
         g2_s = {}
         z = {}
-        h = [lay.tile([P, CHUNK, PACK], BF16, name="h%d" % c, align_bytes=64, offset=H0 + 4096 * c) for c in range(chunks - 1)]
+        h_at = (H0, H0 + 4096, H0 + 8192)
+        h = {}
         h_w = [keep.tile([P, CHUNK], U32, name="h_w%d" % c, align_bytes=64) for c in range(chunks)]
         h_s = [keep.tile([P, CHUNK], U8, name="h_s%d" % c, align_bytes=64) for c in range(chunks)]
 
@@ -120,43 +121,52 @@ def tile_list_kg_relu_none_kernel(
                         start=start, stop=stop,
                     )
 
+        z_bank = (0, 2, 4, 0)
+
         def open_sum(c, s):
-            z[c, s] = banks.tile([P, PACK, SUB], F32, name="z%d_%d" % (c, s), tag="bank%d" % (2 * (c % 2) + s))
+            z[c, s] = banks.tile([P, PACK, SUB], F32, name="z%d_%d" % (c, s), tag="bank%d" % (z_bank[c] + s))
             passes(c, s, 2 if c == 3 else 1, True)
 
-        def close_sum(c, s, on_vector):
-            cols = slice(s * SUB, (s + 1) * SUB)
+        def close_sum(c, s):
             passes(c, s, 1 if c == 3 else 2, False)
+
+        def relu(c, s, on_vector):
+            if s == 0:
+                h[c] = lay.tile([P, CHUNK, PACK], BF16, name="h%d" % c, align_bytes=64, offset=h_at[c])
+            cols = slice(s * SUB, (s + 1) * SUB)
             src = z[c, s][:].rearrange("p t j -> p j t")
             if on_vector:
                 nc.vector.tensor_scalar_max(h[c][:, cols, :], src, 0.0)
             else:
                 nc.scalar.activation(out=h[c][:, cols, :], in_=src, func=RELU)
 
-        def score(c, lo, width, bank):
-            cols = slice(lo, lo + width)
+        def quantise(c):
             nc.vector.quantize_mx(
-                out=h_w[c][:, cols].bitcast(E4M3), scales=h_s[c][:, cols],
-                in_=h[c][:, cols, :].rearrange("p j t -> p (j t)"),
+                out=h_w[c][:].bitcast(E4M3), scales=h_s[c][:], in_=h[c][:].rearrange("p j t -> p (j t)"),
             )
-            y = banks.tile([P, 2, width], F32, name="y%d_%d" % (c, lo), tag="bank%d" % bank)
-            for u in range(2):
-                nc.tensor.matmul_mx(
-                    out=y[:, u, :], lhsT=en_w[:, u * 64 : (u + 1) * 64].bitcast(E2M1),
-                    lhsT_scale=en_s[:].bitcast(U8)[:, u * P : (u + 1) * P],
-                    rhs=h_w[c][:, cols].bitcast(E4M3), rhs_scale=h_s[c][:, cols],
-                    start=True, stop=True,
-                )
-            return y
 
-        def store(y, c, lo, width, on_vector, queue):
-            res = keep.tile([P, 2, width], F32, name="res%d_%d" % (c, lo))
+        def score(words, scales, u, y):
+            nc.tensor.matmul_mx(
+                out=y, lhsT=en_w[:, u * 64 : (u + 1) * 64].bitcast(E2M1),
+                lhsT_scale=en_s[:].bitcast(U8)[:, u * P : (u + 1) * P],
+                rhs=words.bitcast(E4M3), rhs_scale=scales,
+                start=True, stop=True,
+            )
+
+        def score_halves(c, bank_a, bank_b):
+            ys = []
+            for u, bank in enumerate((bank_a, bank_b)):
+                y = banks.tile([P, CHUNK], F32, name="y%d_%d" % (c, u), tag="bank%d" % bank)
+                score(h_w[c][:], h_s[c][:], u, y[:])
+                ys.append(y)
+            return ys
+
+        def store_half(y, c, u, res, on_vector, queue):
             if on_vector:
                 nc.vector.tensor_copy(res[:], y[:])
             else:
                 nc.scalar.copy(res[:], y[:])
-            j0 = c * CHUNK + lo
-            queue.dma_start(out=out.rearrange("(u p) j -> p u j", p=P)[:, :, j0 : j0 + width], in_=res[:])
+            queue.dma_start(out=out[u * P : (u + 1) * P, c * CHUNK : (c + 1) * CHUNK], in_=res[:])
 
         def deal_wa():
             nc.vector.tensor_copy(
@@ -175,39 +185,74 @@ def tile_list_kg_relu_none_kernel(
         deal_scales(wa_s, was_raw)
         deal_wb()
         deal_scales(wb_s, wbs_raw)
-        first = gather("g1_first", U32, A - 1536, tab1_w, list1, 0, 2 * CHUNK)
-        g1_w[0] = first[:, 0:CHUNK]
-        g1_w[1] = first[:, CHUNK:]
-        g1_w[2] = gather("g1_w2", U32, A + 512, tab1_w, list1, 2 * CHUNK, CHUNK)
-        g2_s[0] = gather("g2_s0", U8, A + 1536, tab2_s, list2, 0, J // 2)
-        for c in range(2):
+        warm = banks.tile([P, 4 * P], F32, name="warm", tag="bank7")
+        nc.tensor.matmul_mx(
+            out=warm[:], lhsT=wa_w[:, 0:P].bitcast(E2M1), lhsT_scale=g1_s[:, 0:P],
+            rhs=tab1_w[:, 0 : 4 * P].bitcast(E4M3), rhs_scale=g1_s[:, 0 : 4 * P], start=True, stop=True,
+        )
+        g1_w[0] = gather("g1_w0", U32, 3072, tab1_w, list1, 0, CHUNK)
+        pair = gather("g1_w12", U32, A + 2048, tab1_w, list1, CHUNK, 2 * CHUNK)
+        g1_w[1] = pair[:, 0:CHUNK]
+        g1_w[2] = pair[:, CHUNK:]
+        g2_s[0] = gather("g2_s0", U8, 0, tab2_s, list2, 0, J // 2)
+        for c in range(3):
             open_sum(c, 0)
             open_sum(c, 1)
-        g2_w[0] = gather("g2_w0", U32, B - 2048, tab2_w, list2, 0, CHUNK)
-        g2_w[1] = gather("g2_w1", U32, B - 1024, tab2_w, list2, CHUNK, CHUNK)
-        for c in range(2):
-            close_sum(c, 0, False)
-            close_sum(c, 1, False)
-        g2_w[2] = gather("g2_w2", U32, 1024, tab2_w, list2, 2 * CHUNK, CHUNK)
-        g2_s[1] = gather("g2_s1", U8, A - 1024, tab2_s, list2, J // 2, J // 2)
-        g2_w[3] = gather("g2_w3", U32, A - 2048, tab2_w, list2, 3 * CHUNK, CHUNK)
-        open_sum(2, 0)
-        open_sum(2, 1)
-        close_sum(2, 0, False)
-        close_sum(2, 1, False)
-        y0 = score(0, 0, CHUNK, 4)
-        y1 = score(1, 0, CHUNK, 5)
-        g1_w[3] = gather("g1_w3", U32, H0 + 4096, tab1_w, list1, 3 * CHUNK, CHUNK)
-        store(y0, 0, 0, CHUNK, False, nc.sync)
+        g2_w[0] = gather("g2_w0", U32, B - 1024, tab2_w, list2, 0, CHUNK)
+        pair = gather("g2_w12", U32, 1024, tab2_w, list2, CHUNK, 2 * CHUNK)
+        g2_w[1] = pair[:, 0:CHUNK]
+        g2_w[2] = pair[:, CHUNK:]
+        g2_s[1] = gather("g2_s1", U8, A + 3072, tab2_s, list2, J // 2, J // 2)
+        g2_w[3] = gather("g2_w3", U32, A + 2048, tab2_w, list2, 3 * CHUNK, CHUNK)
+        for c in range(3):
+            for s in range(2):
+                close_sum(c, s)
+                relu(c, s, False)
         open_sum(3, 0)
         open_sum(3, 1)
-        h.append(lay.tile([P, CHUNK, PACK], BF16, name="h3", align_bytes=64, offset=H0 + 4096 * 3))
-        close_sum(3, 0, True)
-        close_sum(3, 1, False)
-        y2 = score(2, 0, CHUNK, 6)
-        y3 = score(3, 0, SUB, 7)
-        y4 = score(3, SUB, SUB, 0)
-        store(y1, 1, 0, CHUNK, False, nc.sync)
-        store(y2, 2, 0, CHUNK, False, nc.sync)
-        store(y3, 3, 0, SUB, False, nc.scalar)
-        store(y4, 3, SUB, SUB, True, nc.sync)
+        quantise(0)
+        y0 = banks.tile([P, 2, CHUNK], F32, name="y0", tag="bank6")
+        for u in range(2):
+            score(h_w[0][:], h_s[0][:], u, y0[:, u, :])
+        quantise(1)
+        y1 = score_halves(1, 7, 2)
+        g1_w[3] = gather("g1_w3", U32, h_at[1], tab1_w, list1, 3 * CHUNK, CHUNK)
+        close_sum(3, 0)
+        close_sum(3, 1)
+        res0 = keep.tile([P, 2, CHUNK], F32, name="res0")
+        nc.scalar.copy(res0[:], y0[:])
+        nc.sync.dma_start(out=out.rearrange("(u p) j -> p u j", p=P)[:, :, 0:CHUNK], in_=res0[:])
+        store_half(y1[1], 1, 1, keep.tile([P, CHUNK], F32, name="res1b"), False, nc.sync)
+        quantise(2)
+        y2 = banks.tile([P, 2, CHUNK], F32, name="y2", tag="bank3")
+        for u in range(2):
+            score(h_w[2][:], h_s[2][:], u, y2[:, u, :])
+        last = [
+            lay.tile([P, SUB, PACK], BF16, name="h3a", align_bytes=64, offset=h_at[2] + 6144),
+            lay.tile([P, SUB, PACK], BF16, name="h3b", align_bytes=64, offset=h_at[2] + 4096),
+        ]
+        nc.vector.tensor_scalar_max(last[0][:], z[3, 0][:].rearrange("p t j -> p j t"), 0.0)
+        nc.scalar.activation(out=last[1][:], in_=z[3, 1][:].rearrange("p t j -> p j t"), func=RELU)
+        res1a = keep.tile([P, CHUNK], F32, name="res1a")
+        store_half(y1[0], 1, 0, res1a, True, nc.sync)
+        y3 = []
+        for s, bank in enumerate((5, 6)):
+            cols = slice(s * SUB, (s + 1) * SUB)
+            nc.vector.quantize_mx(
+                out=h_w[3][:, cols].bitcast(E4M3), scales=h_s[3][:, cols], in_=last[s][:].rearrange("p j t -> p (j t)"),
+            )
+            y = banks.tile([P, 2, SUB], F32, name="y3_%d" % s, tag="bank%d" % bank)
+            for u in range(2):
+                score(h_w[3][:, cols], h_s[3][:, cols], u, y[:, u, :])
+            y3.append(y)
+        res2 = keep.tile([P, 2, CHUNK], F32, name="res2")
+        nc.scalar.copy(res2[:], y2[:])
+        nc.sync.dma_start(out=out.rearrange("(u p) j -> p u j", p=P)[:, :, 2 * CHUNK : 3 * CHUNK], in_=res2[:])
+        for s in range(2):
+            res = keep.tile([P, 2, SUB], F32, name="res3_%d" % s)
+            if s == 1:
+                nc.vector.tensor_copy(res[:], y3[s][:])
+            else:
+                nc.scalar.copy(res[:], y3[s][:])
+            j0 = 3 * CHUNK + s * SUB
+            (nc.scalar, nc.sync)[s].dma_start(out=out.rearrange("(u p) j -> p u j", p=P)[:, :, j0 : j0 + SUB], in_=res[:])

@@ -61,9 +61,9 @@ def tile_list_kg_relu_none_kernel(
         both = (nc.sync, nc.scalar)
 
         nc.vector.memset(tab1_s[:], 0)
-        nc.vector.memset(was_raw[:], 0)
-        nc.vector.memset(tab2_s[:], 0)
-        nc.vector.memset(wbs_raw[:], 0)
+        for plane, words in ((was_raw, R // 4), (tab2_s, T // 4), (wbs_raw, R // 4)):
+            nc.vector.memset(plane[:, 0 : words - 1], 0)
+            nc.vector.memset(plane[:, words - 1 : words], 0)
 
         nc.scalar.dma_start(out=wa_raw[:], in_=wa_words[0].bitcast(I32))
         nc.sync.dma_start(list1[:], offs)
@@ -76,7 +76,7 @@ def tile_list_kg_relu_none_kernel(
         nc.sync.dma_start(list2[:], offs2)
         load_scales(both, was_raw[:], 0, wa_scales)
         load_scales(both, tab2_s[:], ROW2, tab2_scales)
-        load_scales(both, wbs_raw[:], ROW2, wb_scales)
+        load_scales(both, wbs_raw[:], 2 * ROW2, wb_scales)
         load_scales((nc.sync,), en_s[:], 0, en_scales)
 
         g1_s = keep.tile([P, J], U8, name="g1_s", tag="early", align_bytes=64)
@@ -116,7 +116,7 @@ def tile_list_kg_relu_none_kernel(
                 else:
                     j0 = (c % 2) * CHUNK + s * SUB
                     nc.tensor.matmul_mx(
-                        out=z[c, s][:, t, :], lhsT=wb_w[:, rows].bitcast(E4M3), lhsT_scale=wb_s[ROW2:P, rows],
+                        out=z[c, s][:, t, :], lhsT=wb_w[:, rows].bitcast(E4M3), lhsT_scale=wb_s[2 * ROW2 : P, rows],
                         rhs=g2_w[c][:, cols].bitcast(E4M3), rhs_scale=g2_s[c // 2][ROW2:P, j0 : j0 + SUB],
                         start=start, stop=stop,
                     )
@@ -125,10 +125,10 @@ def tile_list_kg_relu_none_kernel(
 
         def open_sum(c, s):
             z[c, s] = banks.tile([P, PACK, SUB], F32, name="z%d_%d" % (c, s), tag="bank%d" % (z_bank[c] + s))
-            passes(c, s, 2 if c == 3 else 1, True)
+            passes(c, s, 1, True)
 
         def close_sum(c, s):
-            passes(c, s, 1 if c == 3 else 2, False)
+            passes(c, s, 2, False)
 
         def relu(c, s, on_vector):
             if s == 0:
@@ -185,11 +185,6 @@ def tile_list_kg_relu_none_kernel(
         deal_scales(wa_s, was_raw)
         deal_wb()
         deal_scales(wb_s, wbs_raw)
-        warm = banks.tile([P, 4 * P], F32, name="warm", tag="bank7")
-        nc.tensor.matmul_mx(
-            out=warm[:], lhsT=wa_w[:, 0:P].bitcast(E2M1), lhsT_scale=g1_s[:, 0:P],
-            rhs=tab1_w[:, 0 : 4 * P].bitcast(E4M3), rhs_scale=g1_s[:, 0 : 4 * P], start=True, stop=True,
-        )
         g1_w[0] = gather("g1_w0", U32, 3072, tab1_w, list1, 0, CHUNK)
         pair = gather("g1_w12", U32, A + 2048, tab1_w, list1, CHUNK, 2 * CHUNK)
         g1_w[1] = pair[:, 0:CHUNK]
@@ -199,11 +194,10 @@ def tile_list_kg_relu_none_kernel(
             open_sum(c, 0)
             open_sum(c, 1)
         g2_w[0] = gather("g2_w0", U32, B - 1024, tab2_w, list2, 0, CHUNK)
-        pair = gather("g2_w12", U32, 1024, tab2_w, list2, CHUNK, 2 * CHUNK)
-        g2_w[1] = pair[:, 0:CHUNK]
-        g2_w[2] = pair[:, CHUNK:]
+        g2_w[1] = gather("g2_w1", U32, 1024, tab2_w, list2, CHUNK, CHUNK)
+        g2_w[2] = gather("g2_w2", U32, 2048, tab2_w, list2, 2 * CHUNK, CHUNK)
         g2_s[1] = gather("g2_s1", U8, A + 3072, tab2_s, list2, J // 2, J // 2)
-        g2_w[3] = gather("g2_w3", U32, A + 2048, tab2_w, list2, 3 * CHUNK, CHUNK)
+        g1_w[3] = gather("g1_w3", U32, A + 2048, tab1_w, list1, 3 * CHUNK, CHUNK)
         for c in range(3):
             for s in range(2):
                 close_sum(c, s)
@@ -214,27 +208,29 @@ def tile_list_kg_relu_none_kernel(
         y0 = banks.tile([P, 2, CHUNK], F32, name="y0", tag="bank6")
         for u in range(2):
             score(h_w[0][:], h_s[0][:], u, y0[:, u, :])
-        quantise(1)
-        y1 = score_halves(1, 7, 2)
-        g1_w[3] = gather("g1_w3", U32, h_at[1], tab1_w, list1, 3 * CHUNK, CHUNK)
+        g2_w[3] = gather("g2_w3", U32, h_at[0], tab2_w, list2, 3 * CHUNK, CHUNK)
         close_sum(3, 0)
         close_sum(3, 1)
+        quantise(1)
+        y1 = banks.tile([P, 2, CHUNK], F32, name="y1", tag="bank7")
+        for u in range(2):
+            score(h_w[1][:], h_s[1][:], u, y1[:, u, :])
         res0 = keep.tile([P, 2, CHUNK], F32, name="res0")
         nc.scalar.copy(res0[:], y0[:])
         nc.sync.dma_start(out=out.rearrange("(u p) j -> p u j", p=P)[:, :, 0:CHUNK], in_=res0[:])
-        store_half(y1[1], 1, 1, keep.tile([P, CHUNK], F32, name="res1b"), False, nc.sync)
         quantise(2)
         y2 = banks.tile([P, 2, CHUNK], F32, name="y2", tag="bank3")
         for u in range(2):
             score(h_w[2][:], h_s[2][:], u, y2[:, u, :])
         last = [
-            lay.tile([P, SUB, PACK], BF16, name="h3a", align_bytes=64, offset=h_at[2] + 6144),
+            lay.tile([P, SUB, PACK], BF16, name="h3a", align_bytes=64, offset=h_at[1]),
             lay.tile([P, SUB, PACK], BF16, name="h3b", align_bytes=64, offset=h_at[2] + 4096),
         ]
         nc.vector.tensor_scalar_max(last[0][:], z[3, 0][:].rearrange("p t j -> p j t"), 0.0)
         nc.scalar.activation(out=last[1][:], in_=z[3, 1][:].rearrange("p t j -> p j t"), func=RELU)
-        res1a = keep.tile([P, CHUNK], F32, name="res1a")
-        store_half(y1[0], 1, 0, res1a, True, nc.sync)
+        res1 = keep.tile([P, 2, CHUNK], F32, name="res1")
+        nc.scalar.copy(res1[:], y1[:])
+        nc.sync.dma_start(out=out.rearrange("(u p) j -> p u j", p=P)[:, :, CHUNK : 2 * CHUNK], in_=res1[:])
         y3 = []
         for s, bank in enumerate((5, 6)):
             cols = slice(s * SUB, (s + 1) * SUB)

@@ -114,10 +114,9 @@ def tile_list_kg_relu_none_kernel(
                         start=start, stop=stop,
                     )
                 else:
-                    j0 = (c % 2) * CHUNK + s * SUB
                     nc.tensor.matmul_mx(
                         out=z[c, s][:, t, :], lhsT=wb_w[:, rows].bitcast(E4M3), lhsT_scale=wb_s[2 * ROW2 : P, rows],
-                        rhs=g2_w[c][:, cols].bitcast(E4M3), rhs_scale=g2_s[c // 2][ROW2:P, j0 : j0 + SUB],
+                        rhs=g2_w[c][:, cols].bitcast(E4M3), rhs_scale=g2_s[c][ROW2:P, cols],
                         start=start, stop=stop,
                     )
 
@@ -125,10 +124,10 @@ def tile_list_kg_relu_none_kernel(
 
         def open_sum(c, s):
             z[c, s] = banks.tile([P, PACK, SUB], F32, name="z%d_%d" % (c, s), tag="bank%d" % (z_bank[c] + s))
-            passes(c, s, 1, True)
+            passes(c, s, 2 if c == 2 else 1, True)
 
         def close_sum(c, s):
-            passes(c, s, 2, False)
+            passes(c, s, 1 if c == 2 else 2, False)
 
         def relu(c, s, on_vector):
             if s == 0:
@@ -185,21 +184,26 @@ def tile_list_kg_relu_none_kernel(
         deal_scales(wa_s, was_raw)
         deal_wb()
         deal_scales(wb_s, wbs_raw)
-        g1_w[0] = gather("g1_w0", U32, 3072, tab1_w, list1, 0, CHUNK)
-        pair = gather("g1_w12", U32, A + 2048, tab1_w, list1, CHUNK, 2 * CHUNK)
-        g1_w[1] = pair[:, 0:CHUNK]
-        g1_w[2] = pair[:, CHUNK:]
-        g2_s[0] = gather("g2_s0", U8, 0, tab2_s, list2, 0, J // 2)
-        for c in range(3):
+        pair = gather("g1_w01", U32, A + 2048, tab1_w, list1, 0, 2 * CHUNK)
+        g1_w[0] = pair[:, 0:CHUNK]
+        g1_w[1] = pair[:, CHUNK:]
+        g1_w[2] = gather("g1_w2", U32, 3072, tab1_w, list1, 2 * CHUNK, CHUNK)
+        pair = gather("g2_s01", U8, 0, tab2_s, list2, 0, 2 * CHUNK)
+        g2_s[0] = pair[:, 0:CHUNK]
+        g2_s[1] = pair[:, CHUNK:]
+        for c in range(2):
             open_sum(c, 0)
             open_sum(c, 1)
         g2_w[0] = gather("g2_w0", U32, B - 1024, tab2_w, list2, 0, CHUNK)
         g2_w[1] = gather("g2_w1", U32, 1024, tab2_w, list2, CHUNK, CHUNK)
         g2_w[2] = gather("g2_w2", U32, 2048, tab2_w, list2, 2 * CHUNK, CHUNK)
-        g2_s[1] = gather("g2_s1", U8, A + 3072, tab2_s, list2, J // 2, J // 2)
+        g2_s[2] = gather("g2_s2", U8, A + 3072, tab2_s, list2, 2 * CHUNK, CHUNK)
         g1_w[3] = gather("g1_w3", U32, A + 2048, tab1_w, list1, 3 * CHUNK, CHUNK)
+        g2_s[3] = gather("g2_s3", U8, A + 3328, tab2_s, list2, 3 * CHUNK, CHUNK)
         for c in range(3):
             for s in range(2):
+                if c == 2:
+                    open_sum(c, s)
                 close_sum(c, s)
                 relu(c, s, False)
         open_sum(3, 0)
@@ -212,25 +216,22 @@ def tile_list_kg_relu_none_kernel(
         close_sum(3, 0)
         close_sum(3, 1)
         quantise(1)
-        y1 = banks.tile([P, 2, CHUNK], F32, name="y1", tag="bank7")
+        y1 = score_halves(1, 7, 2)
         for u in range(2):
-            score(h_w[1][:], h_s[1][:], u, y1[:, u, :])
-        res0 = keep.tile([P, 2, CHUNK], F32, name="res0")
-        nc.scalar.copy(res0[:], y0[:])
-        nc.sync.dma_start(out=out.rearrange("(u p) j -> p u j", p=P)[:, :, 0:CHUNK], in_=res0[:])
+            store_half(y0[:, u, :], 0, u, keep.tile([P, CHUNK], F32, name="res0_%d" % u), False, nc.sync)
         quantise(2)
         y2 = banks.tile([P, 2, CHUNK], F32, name="y2", tag="bank3")
         for u in range(2):
             score(h_w[2][:], h_s[2][:], u, y2[:, u, :])
         last = [
-            lay.tile([P, SUB, PACK], BF16, name="h3a", align_bytes=64, offset=h_at[1]),
+            lay.tile([P, SUB, PACK], BF16, name="h3a", align_bytes=64, offset=h_at[2]),
             lay.tile([P, SUB, PACK], BF16, name="h3b", align_bytes=64, offset=h_at[2] + 4096),
         ]
         nc.vector.tensor_scalar_max(last[0][:], z[3, 0][:].rearrange("p t j -> p j t"), 0.0)
         nc.scalar.activation(out=last[1][:], in_=z[3, 1][:].rearrange("p t j -> p j t"), func=RELU)
-        res1 = keep.tile([P, 2, CHUNK], F32, name="res1")
-        nc.scalar.copy(res1[:], y1[:])
-        nc.sync.dma_start(out=out.rearrange("(u p) j -> p u j", p=P)[:, :, CHUNK : 2 * CHUNK], in_=res1[:])
+        res1a = lay.tile([P, CHUNK], F32, name="res1a", align_bytes=64, offset=h_at[2] + 1024)
+        store_half(y1[0], 1, 0, res1a, True, nc.sync)
+        store_half(y1[1], 1, 1, keep.tile([P, CHUNK], F32, name="res1b"), False, nc.sync)
         y3 = []
         for s, bank in enumerate((5, 6)):
             cols = slice(s * SUB, (s + 1) * SUB)
@@ -241,9 +242,8 @@ def tile_list_kg_relu_none_kernel(
             for u in range(2):
                 score(h_w[3][:, cols], h_s[3][:, cols], u, y[:, u, :])
             y3.append(y)
-        res2 = keep.tile([P, 2, CHUNK], F32, name="res2")
-        nc.scalar.copy(res2[:], y2[:])
-        nc.sync.dma_start(out=out.rearrange("(u p) j -> p u j", p=P)[:, :, 2 * CHUNK : 3 * CHUNK], in_=res2[:])
+        for u in range(2):
+            store_half(y2[:, u, :], 2, u, keep.tile([P, CHUNK], F32, name="res2_%d" % u), False, nc.sync)
         for s in range(2):
             res = keep.tile([P, 2, SUB], F32, name="res3_%d" % s)
             if s == 1:

@@ -219,7 +219,12 @@ def tile_list_kg_relu_none_kernel(
         y1 = score_halves(1, 7, 2)
         for u in range(2):
             store_half(y0[:, u, :], 0, u, keep.tile([P, CHUNK], F32, name="res0_%d" % u), False, nc.sync)
-        quantise(2)
+        for s in range(2):
+            cols = slice(s * SUB, (s + 1) * SUB)
+            nc.vector.quantize_mx(
+                out=h_w[2][:, cols].bitcast(E4M3), scales=h_s[2][:, cols],
+                in_=h[2][:, cols, :].rearrange("p j t -> p (j t)"),
+            )
         y2 = banks.tile([P, 2, CHUNK], F32, name="y2", tag="bank3")
         for u in range(2):
             score(h_w[2][:], h_s[2][:], u, y2[:, u, :])

@@ -120,7 +120,7 @@ def tile_list_kg_relu_none_kernel(
                         start=start, stop=stop,
                     )
 
-        z_bank = (0, 2, 4, 0)
+        z_bank = (0, 2, 0, 2)
 
         def open_sum(c, s):
             z[c, s] = banks.tile([P, PACK, SUB], F32, name="z%d_%d" % (c, s), tag="bank%d" % (z_bank[c] + s))
@@ -201,22 +201,23 @@ def tile_list_kg_relu_none_kernel(
         g1_w[3] = gather("g1_w3", U32, A + 2048, tab1_w, list1, 3 * CHUNK, CHUNK)
         g2_s[3] = gather("g2_s3", U8, A + 3328, tab2_s, list2, 3 * CHUNK, CHUNK)
         for c in range(3):
+            if c == 2:
+                open_sum(c, 0)
+                open_sum(c, 1)
             for s in range(2):
-                if c == 2:
-                    open_sum(c, s)
                 close_sum(c, s)
                 relu(c, s, False)
-        open_sum(3, 0)
-        open_sum(3, 1)
         quantise(0)
-        y0 = banks.tile([P, 2, CHUNK], F32, name="y0", tag="bank6")
+        y0 = banks.tile([P, 2, CHUNK], F32, name="y0", tag="bank4")
         for u in range(2):
             score(h_w[0][:], h_s[0][:], u, y0[:, u, :])
-        g2_w[3] = gather("g2_w3", U32, h_at[0], tab2_w, list2, 3 * CHUNK, CHUNK)
+        open_sum(3, 0)
+        open_sum(3, 1)
+        g2_w[3] = gather("g2_w3", U32, 2048, tab2_w, list2, 3 * CHUNK, CHUNK)
         close_sum(3, 0)
         close_sum(3, 1)
         quantise(1)
-        y1 = score_halves(1, 7, 2)
+        y1 = score_halves(1, 5, 6)
         for u in range(2):
             store_half(y0[:, u, :], 0, u, keep.tile([P, CHUNK], F32, name="res0_%d" % u), False, nc.sync)
         for s in range(2):
@@ -225,7 +226,7 @@ def tile_list_kg_relu_none_kernel(
                 out=h_w[2][:, cols].bitcast(E4M3), scales=h_s[2][:, cols],
                 in_=h[2][:, cols, :].rearrange("p j t -> p (j t)"),
             )
-        y2 = banks.tile([P, 2, CHUNK], F32, name="y2", tag="bank3")
+        y2 = banks.tile([P, 2, CHUNK], F32, name="y2", tag="bank7")
         for u in range(2):
             score(h_w[2][:], h_s[2][:], u, y2[:, u, :])
         last = [
@@ -238,7 +239,7 @@ def tile_list_kg_relu_none_kernel(
         store_half(y1[0], 1, 0, res1a, True, nc.sync)
         store_half(y1[1], 1, 1, keep.tile([P, CHUNK], F32, name="res1b"), False, nc.sync)
         y3 = []
-        for s, bank in enumerate((5, 6)):
+        for s, bank in enumerate((0, 1)):
             cols = slice(s * SUB, (s + 1) * SUB)
             nc.vector.quantize_mx(
                 out=h_w[3][:, cols].bitcast(E4M3), scales=h_s[3][:, cols], in_=last[s][:].rearrange("p j t -> p (j t)"),

@@ -207,54 +207,81 @@ def tile_list_kg_relu_none_kernel(
             for s in range(2):
                 close_sum(c, s)
                 relu(c, s, False)
+        def quantise_part(c, s):
+            cols = slice(s * SUB, (s + 1) * SUB)
+            nc.vector.quantize_mx(
+                out=h_w[c][:, cols].bitcast(E4M3), scales=h_s[c][:, cols],
+                in_=h[c][:, cols, :].rearrange("p j t -> p (j t)"),
+            )
+
+        def score_part(c, s, bank):
+            cols = slice(s * SUB, (s + 1) * SUB)
+            y = banks.tile([P, 2, SUB], F32, name="yp%d_%d" % (c, s), tag="bank%d" % bank)
+            for u in range(2):
+                score(h_w[c][:, cols], h_s[c][:, cols], u, y[:, u, :])
+            return y
+
+        def store_part(y, c, s, res, on_vector):
+            if on_vector:
+                nc.vector.tensor_copy(res[:], y[:])
+            else:
+                nc.scalar.copy(res[:], y[:])
+            j0 = c * CHUNK + s * SUB
+            nc.sync.dma_start(out=out.rearrange("(u p) j -> p u j", p=P)[:, :, j0 : j0 + SUB], in_=res[:])
+
         quantise(0)
         y0 = banks.tile([P, 2, CHUNK], F32, name="y0", tag="bank4")
         for u in range(2):
             score(h_w[0][:], h_s[0][:], u, y0[:, u, :])
+        quantise_part(1, 0)
         open_sum(3, 0)
+        y1a = score_part(1, 0, 5)
         open_sum(3, 1)
-        g2_w[3] = gather("g2_w3", U32, 2048, tab2_w, list2, 3 * CHUNK, CHUNK)
+        g2_w[3] = gather("g2_w3", U32, 3072, tab2_w, list2, 3 * CHUNK, CHUNK)
         close_sum(3, 0)
         close_sum(3, 1)
-        quantise(1)
-        y1 = score_halves(1, 5, 6)
+        quantise_part(1, 1)
+        y1b = score_part(1, 1, 6)
         for u in range(2):
             store_half(y0[:, u, :], 0, u, keep.tile([P, CHUNK], F32, name="res0_%d" % u), False, nc.sync)
+        store_part(y1a, 1, 0, keep.tile([P, 2, SUB], F32, name="res1a"), False)
         for s in range(2):
             cols = slice(s * SUB, (s + 1) * SUB)
             nc.vector.quantize_mx(
                 out=h_w[2][:, cols].bitcast(E4M3), scales=h_s[2][:, cols],
                 in_=h[2][:, cols, :].rearrange("p j t -> p (j t)"),
             )
-        y2 = banks.tile([P, 2, CHUNK], F32, name="y2", tag="bank7")
-        for u in range(2):
-            score(h_w[2][:], h_s[2][:], u, y2[:, u, :])
+        y2 = score_halves(2, 7, 4)
         last = [
             lay.tile([P, SUB, PACK], BF16, name="h3a", align_bytes=64, offset=h_at[2]),
             lay.tile([P, SUB, PACK], BF16, name="h3b", align_bytes=64, offset=h_at[2] + 4096),
         ]
         nc.vector.tensor_scalar_max(last[0][:], z[3, 0][:].rearrange("p t j -> p j t"), 0.0)
         nc.scalar.activation(out=last[1][:], in_=z[3, 1][:].rearrange("p t j -> p j t"), func=RELU)
-        res1a = lay.tile([P, CHUNK], F32, name="res1a", align_bytes=64, offset=h_at[2] + 1024)
-        store_half(y1[0], 1, 0, res1a, True, nc.sync)
-        store_half(y1[1], 1, 1, keep.tile([P, CHUNK], F32, name="res1b"), False, nc.sync)
+        res1b = lay.tile([P, 2, SUB], F32, name="res1b", align_bytes=64, offset=h_at[2] + 1024)
+        store_part(y1b, 1, 1, res1b, True)
         y3 = []
-        for s, bank in enumerate((0, 1)):
+        for s in range(2):
             cols = slice(s * SUB, (s + 1) * SUB)
             nc.vector.quantize_mx(
                 out=h_w[3][:, cols].bitcast(E4M3), scales=h_s[3][:, cols], in_=last[s][:].rearrange("p j t -> p (j t)"),
             )
-            y = banks.tile([P, 2, SUB], F32, name="y3_%d" % s, tag="bank%d" % bank)
-            for u in range(2):
-                score(h_w[3][:, cols], h_s[3][:, cols], u, y[:, u, :])
-            y3.append(y)
-        for u in range(2):
-            store_half(y2[:, u, :], 2, u, keep.tile([P, CHUNK], F32, name="res2_%d" % u), False, nc.sync)
-        for s in range(2):
-            res = keep.tile([P, 2, SUB], F32, name="res3_%d" % s)
-            if s == 1:
-                nc.vector.tensor_copy(res[:], y3[s][:])
+            if s == 0:
+                y = banks.tile([P, 2, SUB], F32, name="y3_0", tag="bank0")
+                y3.append(y)
+                parts = [y[:, u, :] for u in range(2)]
             else:
-                nc.scalar.copy(res[:], y3[s][:])
-            j0 = 3 * CHUNK + s * SUB
-            (nc.scalar, nc.sync)[s].dma_start(out=out.rearrange("(u p) j -> p u j", p=P)[:, :, j0 : j0 + SUB], in_=res[:])
+                parts = [banks.tile([P, SUB], F32, name="y3_1%d" % u, tag="bank%d" % (1 + u))[:] for u in range(2)]
+                y3.extend(parts)
+            for u in range(2):
+                score(h_w[3][:, cols], h_s[3][:, cols], u, parts[u])
+        store_half(y2[0], 2, 0, keep.tile([P, CHUNK], F32, name="res2a"), False, nc.sync)
+        store_half(y2[1], 2, 1, keep.tile([P, CHUNK], F32, name="res2b"), False, nc.sync)
+        store_part(y3[0], 3, 0, keep.tile([P, 2, SUB], F32, name="res3"), True)
+        for u in range(2):
+            res = keep.tile([P, SUB], F32, name="res4_%d" % u)
+            if u == 0:
+                nc.vector.tensor_copy(res[:], y3[1 + u])
+            else:
+                nc.scalar.copy(res[:], y3[1 + u])
+            (nc.sync, nc.scalar)[u].dma_start(out=out[u * P : (u + 1) * P, J - SUB : J], in_=res[:])

@@ -124,10 +124,10 @@ def tile_list_kg_relu_none_kernel(
 
         def open_sum(c, s):
             z[c, s] = banks.tile([P, PACK, SUB], F32, name="z%d_%d" % (c, s), tag="bank%d" % (z_bank[c] + s))
-            passes(c, s, 2 if c == 2 else 1, True)
+            passes(c, s, 1, True)
 
         def close_sum(c, s):
-            passes(c, s, 1 if c == 2 else 2, False)
+            passes(c, s, 2, False)
 
         def relu(c, s, on_vector):
             if s == 0:
@@ -201,10 +201,9 @@ def tile_list_kg_relu_none_kernel(
         g1_w[3] = gather("g1_w3", U32, A + 2048, tab1_w, list1, 3 * CHUNK, CHUNK)
         g2_s[3] = gather("g2_s3", U8, A + 3328, tab2_s, list2, 3 * CHUNK, CHUNK)
         for c in range(3):
-            if c == 2:
-                open_sum(c, 0)
-                open_sum(c, 1)
             for s in range(2):
+                if c == 2:
+                    open_sum(c, s)
                 close_sum(c, s)
                 relu(c, s, False)
         def quantise_part(c, s):
@@ -237,7 +236,7 @@ def tile_list_kg_relu_none_kernel(
         open_sum(3, 0)
         y1a = score_part(1, 0, 5)
         open_sum(3, 1)
-        g2_w[3] = gather("g2_w3", U32, 3072, tab2_w, list2, 3 * CHUNK, CHUNK)
+        g2_w[3] = gather("g2_w3", U32, 2048, tab2_w, list2, 3 * CHUNK, CHUNK)
         close_sum(3, 0)
         close_sum(3, 1)
         quantise_part(1, 1)

@@ -96,8 +96,8 @@ def tile_list_kg_relu_none_kernel(
 
         def deal_scales(dealt, raw):
             nc.gpsimd.tensor_copy(
-                dealt[:].rearrange("p (t m) -> p t m", t=PACK),
-                raw[:].bitcast(U8).rearrange("p (m t) -> p t m", t=PACK),
+                dealt[:].rearrange("p (t c m) -> p c t m", t=PACK, m=16),
+                raw[:].bitcast(U8).rearrange("p (c m t) -> p c t m", t=PACK, m=16),
             )
 
         def passes(c, s, table, first):
@@ -175,8 +175,8 @@ def tile_list_kg_relu_none_kernel(
 
         def deal_wb():
             nc.gpsimd.tensor_copy(
-                wb_w[:].rearrange("p (t m) -> p t m", t=PACK),
-                wb_raw[:].rearrange("p (m t) -> p t m", t=PACK),
+                wb_w[:].rearrange("p (t c m) -> p c t m", t=PACK, m=4),
+                wb_raw[:].rearrange("p (c m t) -> p c t m", t=PACK, m=4),
             )
 
         deal_wa()

@@ -18,8 +18,25 @@ RELU = mybir.ActivationFunctionType.Relu
 P = 128
 PACK = 4
 CHUNK = 256
-SUB = 128
-ROW2 = 4
+PART = 128
+LAST = J // CHUNK - 1
+TAB2_FIRST = 4
+WB_FIRST = 8
+LINE = 16
+
+AT_G1_S01 = 0
+AT_G1_S23 = 512
+AT_G2_W1 = 1024
+AT_G2_W2 = 2048
+AT_TAB1_S = 4096
+AT_G2_ROWS = 6144
+AT_G2_W0 = 8192
+AT_TAB2_S = 9216
+AT_H = 11264
+H_STEP = 4096
+AT_G1_W0 = 3072
+AT_G1_W1 = 26624
+ROWS_AT = 112
 
 
 def tile_list_kg_relu_none_kernel(
@@ -27,260 +44,217 @@ def tile_list_kg_relu_none_kernel(
     en_words, en_scales, offs, offs2, out
 ):
     nc = tc.nc
-    chunks = J // CHUNK
 
-    def load_scales(queue, plane, row0, scales):
+    def load_scales(queues, tile, first, scales):
         rows = scales[0].bitcast(I32)
-        for r in range(4):
-            queue[r % len(queue)].dma_start(out=plane[row0 + r : P : 32], in_=rows[r:16:4, :])
+        for i in range(4):
+            queues[i % len(queues)].dma_start(out=tile[first + i : P : 32], in_=rows[i:16:4, :])
 
     with ExitStack() as ctx:
         keep = ctx.enter_context(tc.tile_pool(name="keep", bufs=1))
         lay = ctx.enter_context(tc.tile_pool(name="lay", bufs=1))
         banks = ctx.enter_context(tc.psum_pool(name="banks", bufs=1))
 
-        A = 4096
-        B = 9216
-        H0 = 11264
         list1 = keep.tile([P, J // 16], U16, name="list1")
         list2 = keep.tile([P, J // 16], U16, name="list2")
         tab1_w = keep.tile([P, T], I32, name="tab1_w", align_bytes=64)
         tab2_w = keep.tile([P, T], I32, name="tab2_w", align_bytes=64)
-        tab1_s = lay.tile([P, T // 4], I32, name="tab1_s", align_bytes=64, offset=A)
-        tab2_s = lay.tile([P, T // 4], I32, name="tab2_s", align_bytes=64, offset=B)
-        wa_raw = keep.tile([P, R // 2], I32, name="wa_raw", tag="early", align_bytes=64)
+        tab1_s = lay.tile([P, T // 4], I32, name="tab1_s", align_bytes=64, offset=AT_TAB1_S)
+        tab2_s = lay.tile([P, T // 4], I32, name="tab2_s", align_bytes=64, offset=AT_TAB2_S)
+        wa_raw = keep.tile([P, R // 2], I32, name="wa_raw", align_bytes=64)
         wb_raw = keep.tile([P, R], I32, name="wb_raw", align_bytes=64)
-        was_raw = keep.tile([P, R // 4], I32, name="was_raw", align_bytes=64)
+        was_raw = keep.tile([P, R // 4], I32, name="was_raw", tag="was", align_bytes=64)
         wbs_raw = keep.tile([P, R // 4], I32, name="wbs_raw", align_bytes=64)
-        wa_w = keep.tile([P, R], U16, name="wa_w", align_bytes=64)
+        wa_w = keep.tile([P, 2 * R], U8, name="wa_w", align_bytes=64)
         wb_w = keep.tile([P, R], I32, name="wb_w", align_bytes=64)
         wa_s = keep.tile([P, R], U8, name="wa_s", align_bytes=64)
         wb_s = keep.tile([P, R], U8, name="wb_s", align_bytes=64)
         en_w = keep.tile([P, N // 2], I32, name="en_w", align_bytes=64)
-        en_s = keep.tile([P, N // 4], I32, name="en_s", align_bytes=64)
         both = (nc.sync, nc.scalar)
 
         nc.vector.memset(tab1_s[:], 0)
-        for plane, words in ((was_raw, R // 4), (tab2_s, T // 4), (wbs_raw, R // 4)):
-            nc.vector.memset(plane[:, 0 : words - 1], 0)
-            nc.vector.memset(plane[:, words - 1 : words], 0)
+        for tile, words in ((tab2_s[0:ROWS_AT], T // 4), (was_raw, R // 4), (wbs_raw, R // 4)):
+            nc.vector.memset(tile[:, 0 : words - 1], 0)
+            nc.vector.memset(tile[:, words - 1 : words], 0)
 
-        nc.scalar.dma_start(out=wa_raw[:], in_=wa_words[0].bitcast(I32))
+        nc.sync.dma_start(list2[:], offs2)
+        nc.scalar.dma_start(out=tab2_s[ROWS_AT:P], in_=tab2_scales[0].bitcast(I32))
         nc.sync.dma_start(list1[:], offs)
+        nc.scalar.dma_start(out=wa_raw[:], in_=wa_words[0].bitcast(I32))
         nc.gpsimd.dma_start(out=tab1_w[:], in_=tab_words[0].rearrange("p t i -> p (t i)").bitcast(I32))
         nc.gpsimd.dma_start(out=wb_raw[:], in_=wb_words[0].rearrange("p r i -> p (r i)").bitcast(I32))
-        nc.gpsimd.memset(en_s[:], 0)
         nc.gpsimd.dma_start(out=tab2_w[:], in_=tab2_words[0].rearrange("p t i -> p (t i)").bitcast(I32))
         nc.gpsimd.dma_start(out=en_w[:], in_=en_words[0].bitcast(I32))
         load_scales(both, tab1_s[:], 0, tab_scales)
-        nc.sync.dma_start(list2[:], offs2)
         load_scales(both, was_raw[:], 0, wa_scales)
-        load_scales(both, tab2_s[:], ROW2, tab2_scales)
-        load_scales(both, wbs_raw[:], 2 * ROW2, wb_scales)
-        load_scales((nc.sync,), en_s[:], 0, en_scales)
+        load_scales(both, wbs_raw[:], WB_FIRST, wb_scales)
 
-        g1_s = keep.tile([P, J], U8, name="g1_s", tag="early", align_bytes=64)
+        g1_s = {}
         g1_w = {}
         g2_w = {}
-        g2_s = {}
         z = {}
-        h_at = (H0, H0 + 4096, H0 + 8192)
         h = {}
-        h_w = [keep.tile([P, CHUNK], U32, name="h_w%d" % c, align_bytes=64) for c in range(chunks)]
-        h_s = [keep.tile([P, CHUNK], U8, name="h_s%d" % c, align_bytes=64) for c in range(chunks)]
+        h_w = [keep.tile([P, CHUNK], U32, name="h_w%d" % c, align_bytes=64) for c in range(LAST + 1)]
+        h_s = [keep.tile([P, CHUNK], U8, name="h_s%d" % c, align_bytes=64) for c in range(LAST + 1)]
 
         def gather(name, dtype, at, window, lst, lo, width):
             got = lay.tile([P, width], dtype, name=name, align_bytes=64, offset=at)
             nc.vector.tensor_copy(got[:], window[:].bitcast(dtype).indirect(lst[:, lo // 16 : (lo + width) // 16]))
             return got
 
-        def deal_scales(dealt, raw):
+        def deal_on_gpsimd(dealt, raw, run):
             nc.gpsimd.tensor_copy(
-                dealt[:].rearrange("p (t c m) -> p c t m", t=PACK, m=16),
-                raw[:].bitcast(U8).rearrange("p (c m t) -> p c t m", t=PACK, m=16),
+                dealt.rearrange("p (t c m) -> p c t m", t=PACK, m=run),
+                raw.rearrange("p (c m t) -> p c t m", t=PACK, m=run),
             )
-
-        def passes(c, s, table, first):
-            cols = slice(s * SUB, (s + 1) * SUB)
-            for t in range(PACK):
-                rows = slice(t * P, (t + 1) * P)
-                start = first and t == 0
-                stop = (not first) and t == PACK - 1
-                if table == 1:
-                    j0 = c * CHUNK + s * SUB
-                    nc.tensor.matmul_mx(
-                        out=z[c, s][:, t, :], lhsT=wa_w[:, rows].bitcast(E2M1), lhsT_scale=wa_s[:, rows],
-                        rhs=g1_w[c][:, cols].bitcast(E4M3), rhs_scale=g1_s[:, j0 : j0 + SUB],
-                        start=start, stop=stop,
-                    )
-                else:
-                    nc.tensor.matmul_mx(
-                        out=z[c, s][:, t, :], lhsT=wb_w[:, rows].bitcast(E4M3), lhsT_scale=wb_s[2 * ROW2 : P, rows],
-                        rhs=g2_w[c][:, cols].bitcast(E4M3), rhs_scale=g2_s[c][ROW2:P, cols],
-                        start=start, stop=stop,
-                    )
-
-        z_bank = (0, 2, 0, 2)
 
         def open_sum(c, s):
-            z[c, s] = banks.tile([P, PACK, SUB], F32, name="z%d_%d" % (c, s), tag="bank%d" % (z_bank[c] + s))
-            passes(c, s, 1, True)
+            z[c, s] = banks.tile([P, PACK, PART], F32, name="z%d_%d" % (c, s), tag="bank%d" % (2 * (c % 2) + s))
+            cols = slice(s * PART, (s + 1) * PART)
+            for t in range(PACK):
+                slice_t = slice(t * P, (t + 1) * P)
+                nc.tensor.matmul_mx(
+                    out=z[c, s][:, t, :], lhsT=wa_w[:, 2 * t * P : 2 * (t + 1) * P].bitcast(E2M1),
+                    lhsT_scale=wa_s[:, slice_t],
+                    rhs=g1_w[c][:, cols].bitcast(E4M3), rhs_scale=g1_s[c][:, cols],
+                    start=t == 0, stop=False,
+                )
 
         def close_sum(c, s):
-            passes(c, s, 2, False)
+            cols = slice(s * PART, (s + 1) * PART)
+            j0 = c * CHUNK + s * PART
+            for t in range(PACK):
+                slice_t = slice(t * P, (t + 1) * P)
+                nc.tensor.matmul_mx(
+                    out=z[c, s][:, t, :], lhsT=wb_w[:, slice_t].bitcast(E4M3), lhsT_scale=wb_s[WB_FIRST:P, slice_t],
+                    rhs=g2_w[c][:, cols].bitcast(E4M3), rhs_scale=g2_s[:].bitcast(U8)[TAB2_FIRST:P, j0 : j0 + PART],
+                    start=False, stop=t == PACK - 1,
+                )
 
-        def relu(c, s, on_vector):
-            if s == 0:
-                h[c] = lay.tile([P, CHUNK, PACK], BF16, name="h%d" % c, align_bytes=64, offset=h_at[c])
-            cols = slice(s * SUB, (s + 1) * SUB)
-            src = z[c, s][:].rearrange("p t j -> p j t")
-            if on_vector:
-                nc.vector.tensor_scalar_max(h[c][:, cols, :], src, 0.0)
-            else:
-                nc.scalar.activation(out=h[c][:, cols, :], in_=src, func=RELU)
+        def interleaved(c, s):
+            return z[c, s][:].rearrange("p t j -> p j t")
 
-        def quantise(c):
+        def quantise(c, cols, values):
             nc.vector.quantize_mx(
-                out=h_w[c][:].bitcast(E4M3), scales=h_s[c][:], in_=h[c][:].rearrange("p j t -> p (j t)"),
+                out=h_w[c][:, cols].bitcast(E4M3), scales=h_s[c][:, cols], in_=values.rearrange("p j t -> p (j t)"),
             )
 
-        def score(words, scales, u, y):
+        def quantise_part(c, s):
+            cols = slice(s * PART, (s + 1) * PART)
+            quantise(c, cols, h[c][:, cols, :])
+
+        def score(c, cols, u, y):
             nc.tensor.matmul_mx(
                 out=y, lhsT=en_w[:, u * 64 : (u + 1) * 64].bitcast(E2M1),
                 lhsT_scale=en_s[:].bitcast(U8)[:, u * P : (u + 1) * P],
-                rhs=words.bitcast(E4M3), rhs_scale=scales,
+                rhs=h_w[c][:, cols].bitcast(E4M3), rhs_scale=h_s[c][:, cols],
                 start=True, stop=True,
             )
 
-        def score_halves(c, bank_a, bank_b):
-            ys = []
-            for u, bank in enumerate((bank_a, bank_b)):
-                y = banks.tile([P, CHUNK], F32, name="y%d_%d" % (c, u), tag="bank%d" % bank)
-                score(h_w[c][:], h_s[c][:], u, y[:])
-                ys.append(y)
-            return ys
+        def score_part(c, s, name, bank):
+            y = banks.tile([P, 2, PART], F32, name=name, tag="bank%d" % bank)
+            for u in range(2):
+                score(c, slice(s * PART, (s + 1) * PART), u, y[:, u, :])
+            return y
 
-        def store_half(y, c, u, res, on_vector, queue):
-            if on_vector:
-                nc.vector.tensor_copy(res[:], y[:])
-            else:
-                nc.scalar.copy(res[:], y[:])
-            queue.dma_start(out=out[u * P : (u + 1) * P, c * CHUNK : (c + 1) * CHUNK], in_=res[:])
+        def store_rows(y, c, u, res):
+            nc.scalar.copy(res[:], y)
+            nc.sync.dma_start(out=out[u * P : (u + 1) * P, c * CHUNK : (c + 1) * CHUNK], in_=res[:])
 
-        def deal_wa():
-            nc.vector.tensor_copy(
-                wa_w[:].rearrange("p (t m) -> p t m", t=PACK),
-                wa_raw[:].bitcast(U16).rearrange("p (m t) -> p t m", t=PACK),
+        def store_part(copy, y, c, s, res):
+            copy(res[:], y[:])
+            j0 = c * CHUNK + s * PART
+            nc.sync.dma_start(out=out.rearrange("(u p) j -> p u j", p=P)[:, :, j0 : j0 + PART], in_=res[:])
+
+        whole = slice(0, CHUNK)
+
+        g2_rows = gather("g2_rows", U8, AT_G2_ROWS, tab2_s, list2, 0, J)
+        g2_s = lay.tile([P, J // 4], I32, name="g2_s", align_bytes=64, offset=AT_TAB2_S)
+        for i in range(4):
+            both[i % 2].dma_start(
+                out=g2_s[TAB2_FIRST + i : P : 32], in_=g2_rows[:].bitcast(I32)[ROWS_AT + i : P : 4]
             )
+        nc.vector.tensor_copy(
+            wa_w[:].bitcast(U16).rearrange("p (t m) -> p t m", t=PACK),
+            wa_raw[:].bitcast(U16).rearrange("p (m t) -> p t m", t=PACK),
+        )
+        deal_on_gpsimd(wa_s[:], was_raw[:].bitcast(U8), LINE)
+        deal_on_gpsimd(wb_w[:], wb_raw[:], LINE // 4)
+        deal_on_gpsimd(wb_s[:], wbs_raw[:].bitcast(U8), LINE)
+        en_s = keep.tile([P, N // 4], I32, name="en_s", tag="was", align_bytes=64)
+        nc.gpsimd.memset(en_s[:], 0)
+        load_scales((nc.sync,), en_s[:], 0, en_scales)
 
-        def deal_wb():
-            nc.gpsimd.tensor_copy(
-                wb_w[:].rearrange("p (t c m) -> p c t m", t=PACK, m=4),
-                wb_raw[:].rearrange("p (c m t) -> p c t m", t=PACK, m=4),
-            )
-
-        deal_wa()
-        nc.vector.tensor_copy(g1_s[:], tab1_s[:].bitcast(U8).indirect(list1[:]))
-        deal_scales(wa_s, was_raw)
-        deal_wb()
-        deal_scales(wb_s, wbs_raw)
-        pair = gather("g1_w01", U32, A + 2048, tab1_w, list1, 0, 2 * CHUNK)
-        g1_w[0] = pair[:, 0:CHUNK]
-        g1_w[1] = pair[:, CHUNK:]
-        g1_w[2] = gather("g1_w2", U32, 3072, tab1_w, list1, 2 * CHUNK, CHUNK)
-        pair = gather("g2_s01", U8, 0, tab2_s, list2, 0, 2 * CHUNK)
-        g2_s[0] = pair[:, 0:CHUNK]
-        g2_s[1] = pair[:, CHUNK:]
+        pair = gather("g1_s01", U8, AT_G1_S01, tab1_s, list1, 0, 2 * CHUNK)
+        g1_s[0] = pair[:, 0:CHUNK]
+        g1_s[1] = pair[:, CHUNK:]
+        g1_w[0] = gather("g1_w0", U32, AT_G1_W0, tab1_w, list1, 0, CHUNK)
+        g1_w[1] = gather("g1_w1", U32, AT_G1_W1, tab1_w, list1, CHUNK, CHUNK)
+        pair = gather("g1_s23", U8, AT_G1_S23, tab1_s, list1, 2 * CHUNK, 2 * CHUNK)
+        g1_s[2] = pair[:, 0:CHUNK]
+        g1_s[LAST] = pair[:, CHUNK:]
         for c in range(2):
             open_sum(c, 0)
             open_sum(c, 1)
-        g2_w[0] = gather("g2_w0", U32, B - 1024, tab2_w, list2, 0, CHUNK)
-        g2_w[1] = gather("g2_w1", U32, 1024, tab2_w, list2, CHUNK, CHUNK)
-        g2_w[2] = gather("g2_w2", U32, 2048, tab2_w, list2, 2 * CHUNK, CHUNK)
-        g2_s[2] = gather("g2_s2", U8, A + 3072, tab2_s, list2, 2 * CHUNK, CHUNK)
-        g1_w[3] = gather("g1_w3", U32, A + 2048, tab1_w, list1, 3 * CHUNK, CHUNK)
-        g2_s[3] = gather("g2_s3", U8, A + 3328, tab2_s, list2, 3 * CHUNK, CHUNK)
-        for c in range(3):
+        g2_w[0] = gather("g2_w0", U32, AT_G2_W0, tab2_w, list2, 0, CHUNK)
+        g2_w[1] = gather("g2_w1", U32, AT_G2_W1, tab2_w, list2, CHUNK, CHUNK)
+        g2_w[2] = gather("g2_w2", U32, AT_G2_W2, tab2_w, list2, 2 * CHUNK, CHUNK)
+        g1_w[2] = gather("g1_w2", U32, AT_G1_W1 - 2 * CHUNK, tab1_w, list1, 2 * CHUNK, CHUNK)
+        g1_w[LAST] = gather("g1_w3", U32, AT_G1_W1 + 2 * CHUNK, tab1_w, list1, LAST * CHUNK, CHUNK)
+
+        for c in range(LAST):
             for s in range(2):
                 if c == 2:
                     open_sum(c, s)
                 close_sum(c, s)
-                relu(c, s, False)
-        def quantise_part(c, s):
-            cols = slice(s * SUB, (s + 1) * SUB)
-            nc.vector.quantize_mx(
-                out=h_w[c][:, cols].bitcast(E4M3), scales=h_s[c][:, cols],
-                in_=h[c][:, cols, :].rearrange("p j t -> p (j t)"),
-            )
+                if s == 0:
+                    h[c] = lay.tile([P, CHUNK, PACK], BF16, name="h%d" % c, align_bytes=64, offset=AT_H + c * H_STEP)
+                nc.scalar.activation(out=h[c][:, s * PART : (s + 1) * PART, :], in_=interleaved(c, s), func=RELU)
 
-        def score_part(c, s, bank):
-            cols = slice(s * SUB, (s + 1) * SUB)
-            y = banks.tile([P, 2, SUB], F32, name="yp%d_%d" % (c, s), tag="bank%d" % bank)
-            for u in range(2):
-                score(h_w[c][:, cols], h_s[c][:, cols], u, y[:, u, :])
-            return y
-
-        def store_part(y, c, s, res, on_vector):
-            if on_vector:
-                nc.vector.tensor_copy(res[:], y[:])
-            else:
-                nc.scalar.copy(res[:], y[:])
-            j0 = c * CHUNK + s * SUB
-            nc.sync.dma_start(out=out.rearrange("(u p) j -> p u j", p=P)[:, :, j0 : j0 + SUB], in_=res[:])
-
-        quantise(0)
+        quantise(0, whole, h[0][:])
         y0 = banks.tile([P, 2, CHUNK], F32, name="y0", tag="bank4")
         for u in range(2):
-            score(h_w[0][:], h_s[0][:], u, y0[:, u, :])
+            score(0, whole, u, y0[:, u, :])
         quantise_part(1, 0)
-        open_sum(3, 0)
-        y1a = score_part(1, 0, 5)
-        open_sum(3, 1)
-        g2_w[3] = gather("g2_w3", U32, 2048, tab2_w, list2, 3 * CHUNK, CHUNK)
-        close_sum(3, 0)
-        close_sum(3, 1)
+        open_sum(LAST, 0)
+        y1a = score_part(1, 0, "yp1_0", 5)
+        open_sum(LAST, 1)
+        g2_w[LAST] = gather("g2_w3", U32, AT_G2_W2, tab2_w, list2, LAST * CHUNK, CHUNK)
+        close_sum(LAST, 0)
+        close_sum(LAST, 1)
         quantise_part(1, 1)
-        y1b = score_part(1, 1, 6)
-        for u in range(2):
-            store_half(y0[:, u, :], 0, u, keep.tile([P, CHUNK], F32, name="res0_%d" % u), False, nc.sync)
-        store_part(y1a, 1, 0, keep.tile([P, 2, SUB], F32, name="res1a"), False)
+        y1b = score_part(1, 1, "yp1_1", 6)
+        res0 = keep.tile([P, 2, CHUNK], F32, name="res0")
+        nc.scalar.copy(res0[:], y0[:])
+        nc.sync.dma_start(out=out.rearrange("(u p) j -> p u j", p=P)[:, :, 0:CHUNK], in_=res0[:])
+        store_part(nc.scalar.copy, y1a, 1, 0, keep.tile([P, 2, PART], F32, name="res1a"))
         for s in range(2):
-            cols = slice(s * SUB, (s + 1) * SUB)
-            nc.vector.quantize_mx(
-                out=h_w[2][:, cols].bitcast(E4M3), scales=h_s[2][:, cols],
-                in_=h[2][:, cols, :].rearrange("p j t -> p (j t)"),
-            )
-        y2 = score_halves(2, 7, 4)
-        last = [
-            lay.tile([P, SUB, PACK], BF16, name="h3a", align_bytes=64, offset=h_at[2]),
-            lay.tile([P, SUB, PACK], BF16, name="h3b", align_bytes=64, offset=h_at[2] + 4096),
+            quantise_part(2, s)
+        y2 = []
+        for u, bank in enumerate((7, 4)):
+            y2.append(banks.tile([P, CHUNK], F32, name="y2_%d" % u, tag="bank%d" % bank))
+            score(2, whole, u, y2[u][:])
+
+        at_h2 = AT_H + 2 * H_STEP
+        h_last = [
+            lay.tile([P, PART, PACK], BF16, name="h3a", align_bytes=64, offset=at_h2),
+            lay.tile([P, PART, PACK], BF16, name="h3b", align_bytes=64, offset=at_h2 + H_STEP),
         ]
-        nc.vector.tensor_scalar_max(last[0][:], z[3, 0][:].rearrange("p t j -> p j t"), 0.0)
-        nc.scalar.activation(out=last[1][:], in_=z[3, 1][:].rearrange("p t j -> p j t"), func=RELU)
-        res1b = lay.tile([P, 2, SUB], F32, name="res1b", align_bytes=64, offset=h_at[2] + 1024)
-        store_part(y1b, 1, 1, res1b, True)
-        y3 = []
-        for s in range(2):
-            cols = slice(s * SUB, (s + 1) * SUB)
-            nc.vector.quantize_mx(
-                out=h_w[3][:, cols].bitcast(E4M3), scales=h_s[3][:, cols], in_=last[s][:].rearrange("p j t -> p (j t)"),
-            )
-            if s == 0:
-                y = banks.tile([P, 2, SUB], F32, name="y3_0", tag="bank0")
-                y3.append(y)
-                parts = [y[:, u, :] for u in range(2)]
-            else:
-                parts = [banks.tile([P, SUB], F32, name="y3_1%d" % u, tag="bank%d" % (1 + u))[:] for u in range(2)]
-                y3.extend(parts)
-            for u in range(2):
-                score(h_w[3][:, cols], h_s[3][:, cols], u, parts[u])
-        store_half(y2[0], 2, 0, keep.tile([P, CHUNK], F32, name="res2a"), False, nc.sync)
-        store_half(y2[1], 2, 1, keep.tile([P, CHUNK], F32, name="res2b"), False, nc.sync)
-        store_part(y3[0], 3, 0, keep.tile([P, 2, SUB], F32, name="res3"), True)
+        nc.vector.tensor_scalar_max(h_last[0][:], interleaved(LAST, 0), 0.0)
+        nc.scalar.activation(out=h_last[1][:], in_=interleaved(LAST, 1), func=RELU)
+        res1b = lay.tile([P, 2, PART], F32, name="res1b", align_bytes=64, offset=at_h2 + 2 * PACK * PART)
+        store_part(nc.vector.tensor_copy, y1b, 1, 1, res1b)
+
+        quantise(LAST, slice(0, PART), h_last[0][:])
+        y3a = score_part(LAST, 0, "y3_0", 0)
+        quantise(LAST, slice(PART, CHUNK), h_last[1][:])
+        y3b = [banks.tile([P, PART], F32, name="y3_1%d" % u, tag="bank%d" % (1 + u)) for u in range(2)]
         for u in range(2):
-            res = keep.tile([P, SUB], F32, name="res4_%d" % u)
-            if u == 0:
-                nc.vector.tensor_copy(res[:], y3[1 + u])
-            else:
-                nc.scalar.copy(res[:], y3[1 + u])
-            (nc.sync, nc.scalar)[u].dma_start(out=out[u * P : (u + 1) * P, J - SUB : J], in_=res[:])
+            score(LAST, slice(PART, CHUNK), u, y3b[u][:])
+        store_rows(y2[0][:], 2, 0, keep.tile([P, CHUNK], F32, name="res2a"))
+        store_rows(y2[1][:], 2, 1, keep.tile([P, CHUNK], F32, name="res2b"))
+        store_part(nc.vector.tensor_copy, y3a, LAST, 0, keep.tile([P, 2, PART], F32, name="res3"))
+        for u, (copy, queue) in enumerate(((nc.vector.tensor_copy, nc.sync), (nc.scalar.copy, nc.scalar))):
+            res = keep.tile([P, PART], F32, name="res4_%d" % u)
+            copy(res[:], y3b[u][:])
+            queue.dma_start(out=out[u * P : (u + 1) * P, J - PART : J], in_=res[:])

from contextlib import ExitStack

import concourse.mybir as mybir

K, L, R, N, T, J = 512, 512, 512, 256, 2048, 1024
FLOPS = 2 * J * (K * R + L * R + R * N)

F32 = mybir.dt.float32
BF16 = mybir.dt.bfloat16
I32 = mybir.dt.int32
U32 = mybir.dt.uint32
U16 = mybir.dt.uint16
U8 = mybir.dt.uint8
E4M3 = mybir.dt.float8_e4m3fn_x4
E2M1 = mybir.dt.float4_e2m1fn_x4
RELU = mybir.ActivationFunctionType.Relu

P = 128
PACK = 4
CHUNK = 256
PART = 128
LAST = J // CHUNK - 1
TAB2_FIRST = 4
WB_FIRST = 8
LINE = 16

AT_G1_S01 = 0
AT_G1_S23 = 512
AT_G2_W1 = 1024
AT_G2_W2 = 2048
AT_TAB1_S = 4096
AT_G2_ROWS = 6144
AT_G2_W0 = 8192
AT_TAB2_S = 9216
AT_H = 11264
H_STEP = 4096
AT_G1_W0 = 3072
AT_G1_W1 = 26624
ROWS_AT = 112


def tile_list_kg_relu_none_kernel(
    tc, tab_words, tab_scales, tab2_words, tab2_scales, wa_words, wa_scales, wb_words, wb_scales,
    en_words, en_scales, offs, offs2, out
):
    nc = tc.nc

    def load_scales(queues, tile, first, scales):
        rows = scales[0].bitcast(I32)
        for i in range(4):
            queues[i % len(queues)].dma_start(out=tile[first + i : P : 32], in_=rows[i:16:4, :])

    with ExitStack() as ctx:
        keep = ctx.enter_context(tc.tile_pool(name="keep", bufs=1))
        lay = ctx.enter_context(tc.tile_pool(name="lay", bufs=1))
        banks = ctx.enter_context(tc.psum_pool(name="banks", bufs=1))

        list1 = keep.tile([P, J // 16], U16, name="list1")
        list2 = keep.tile([P, J // 16], U16, name="list2")
        tab1_w = keep.tile([P, T], I32, name="tab1_w", align_bytes=64)
        tab2_w = keep.tile([P, T], I32, name="tab2_w", align_bytes=64)
        tab1_s = lay.tile([P, T // 4], I32, name="tab1_s", align_bytes=64, offset=AT_TAB1_S)
        tab2_s = lay.tile([P, T // 4], I32, name="tab2_s", align_bytes=64, offset=AT_TAB2_S)
        wa_raw = keep.tile([P, R // 2], I32, name="wa_raw", align_bytes=64)
        wb_raw = keep.tile([P, R], I32, name="wb_raw", align_bytes=64)
        was_raw = keep.tile([P, R // 4], I32, name="was_raw", tag="was", align_bytes=64)
        wbs_raw = keep.tile([P, R // 4], I32, name="wbs_raw", align_bytes=64)
        wa_w = keep.tile([P, 2 * R], U8, name="wa_w", align_bytes=64)
        wb_w = keep.tile([P, R], I32, name="wb_w", align_bytes=64)
        wa_s = keep.tile([P, R], U8, name="wa_s", align_bytes=64)
        wb_s = keep.tile([P, R], U8, name="wb_s", align_bytes=64)
        en_w = keep.tile([P, N // 2], I32, name="en_w", align_bytes=64)
        both = (nc.sync, nc.scalar)

        nc.vector.memset(tab1_s[:], 0)
        for tile, words in ((tab2_s[0:ROWS_AT], T // 4), (was_raw, R // 4), (wbs_raw, R // 4)):
            nc.vector.memset(tile[:, 0 : words - 1], 0)
            nc.vector.memset(tile[:, words - 1 : words], 0)

        nc.sync.dma_start(list2[:], offs2)
        nc.scalar.dma_start(out=tab2_s[ROWS_AT:P], in_=tab2_scales[0].bitcast(I32))
        nc.sync.dma_start(list1[:], offs)
        nc.scalar.dma_start(out=wa_raw[:], in_=wa_words[0].bitcast(I32))
        nc.gpsimd.dma_start(out=tab1_w[:], in_=tab_words[0].rearrange("p t i -> p (t i)").bitcast(I32))
        nc.gpsimd.dma_start(out=wb_raw[:], in_=wb_words[0].rearrange("p r i -> p (r i)").bitcast(I32))
        nc.gpsimd.dma_start(out=tab2_w[:], in_=tab2_words[0].rearrange("p t i -> p (t i)").bitcast(I32))
        nc.gpsimd.dma_start(out=en_w[:], in_=en_words[0].bitcast(I32))
        load_scales(both, tab1_s[:], 0, tab_scales)
        load_scales(both, was_raw[:], 0, wa_scales)
        load_scales(both, wbs_raw[:], WB_FIRST, wb_scales)

        g1_s = {}
        g1_w = {}
        g2_w = {}
        z = {}
        h = {}
        h_w = [keep.tile([P, CHUNK], U32, name="h_w%d" % c, align_bytes=64) for c in range(LAST + 1)]
        h_s = [keep.tile([P, CHUNK], U8, name="h_s%d" % c, align_bytes=64) for c in range(LAST + 1)]

        def gather(name, dtype, at, window, lst, lo, width):
            got = lay.tile([P, width], dtype, name=name, align_bytes=64, offset=at)
            nc.vector.tensor_copy(got[:], window[:].bitcast(dtype).indirect(lst[:, lo // 16 : (lo + width) // 16]))
            return got

        def deal_on_gpsimd(dealt, raw, run):
            nc.gpsimd.tensor_copy(
                dealt.rearrange("p (t c m) -> p c t m", t=PACK, m=run),
                raw.rearrange("p (c m t) -> p c t m", t=PACK, m=run),
            )

        def open_sum(c, s):
            z[c, s] = banks.tile([P, PACK, PART], F32, name="z%d_%d" % (c, s), tag="bank%d" % (2 * (c % 2) + s))
            cols = slice(s * PART, (s + 1) * PART)
            for t in range(PACK):
                slice_t = slice(t * P, (t + 1) * P)
                nc.tensor.matmul_mx(
                    out=z[c, s][:, t, :], lhsT=wa_w[:, 2 * t * P : 2 * (t + 1) * P].bitcast(E2M1),
                    lhsT_scale=wa_s[:, slice_t],
                    rhs=g1_w[c][:, cols].bitcast(E4M3), rhs_scale=g1_s[c][:, cols],
                    start=t == 0, stop=False,
                )

        def close_sum(c, s):
            cols = slice(s * PART, (s + 1) * PART)
            j0 = c * CHUNK + s * PART
            for t in range(PACK):
                slice_t = slice(t * P, (t + 1) * P)
                nc.tensor.matmul_mx(
                    out=z[c, s][:, t, :], lhsT=wb_w[:, slice_t].bitcast(E4M3), lhsT_scale=wb_s[WB_FIRST:P, slice_t],
                    rhs=g2_w[c][:, cols].bitcast(E4M3), rhs_scale=g2_s[:].bitcast(U8)[TAB2_FIRST:P, j0 : j0 + PART],
                    start=False, stop=t == PACK - 1,
                )

        def interleaved(c, s):
            return z[c, s][:].rearrange("p t j -> p j t")

        def quantise(c, cols, values):
            nc.vector.quantize_mx(
                out=h_w[c][:, cols].bitcast(E4M3), scales=h_s[c][:, cols], in_=values.rearrange("p j t -> p (j t)"),
            )

        def quantise_part(c, s):
            cols = slice(s * PART, (s + 1) * PART)
            quantise(c, cols, h[c][:, cols, :])

        def score(c, cols, u, y):
            nc.tensor.matmul_mx(
                out=y, lhsT=en_w[:, u * 64 : (u + 1) * 64].bitcast(E2M1),
                lhsT_scale=en_s[:].bitcast(U8)[:, u * P : (u + 1) * P],
                rhs=h_w[c][:, cols].bitcast(E4M3), rhs_scale=h_s[c][:, cols],
                start=True, stop=True,
            )

        def score_part(c, s, name, bank):
            y = banks.tile([P, 2, PART], F32, name=name, tag="bank%d" % bank)
            for u in range(2):
                score(c, slice(s * PART, (s + 1) * PART), u, y[:, u, :])
            return y

        def store_rows(y, c, u, res):
            nc.scalar.copy(res[:], y)
            nc.sync.dma_start(out=out[u * P : (u + 1) * P, c * CHUNK : (c + 1) * CHUNK], in_=res[:])

        def store_part(copy, y, c, s, res):
            copy(res[:], y[:])
            j0 = c * CHUNK + s * PART
            nc.sync.dma_start(out=out.rearrange("(u p) j -> p u j", p=P)[:, :, j0 : j0 + PART], in_=res[:])

        whole = slice(0, CHUNK)

        g2_rows = gather("g2_rows", U8, AT_G2_ROWS, tab2_s, list2, 0, J)
        g2_s = lay.tile([P, J // 4], I32, name="g2_s", align_bytes=64, offset=AT_TAB2_S)
        for i in range(4):
            both[i % 2].dma_start(
                out=g2_s[TAB2_FIRST + i : P : 32], in_=g2_rows[:].bitcast(I32)[ROWS_AT + i : P : 4]
            )
        nc.vector.tensor_copy(
            wa_w[:].bitcast(U16).rearrange("p (t m) -> p t m", t=PACK),
            wa_raw[:].bitcast(U16).rearrange("p (m t) -> p t m", t=PACK),
        )
        deal_on_gpsimd(wa_s[:], was_raw[:].bitcast(U8), LINE)
        deal_on_gpsimd(wb_w[:], wb_raw[:], LINE // 4)
        deal_on_gpsimd(wb_s[:], wbs_raw[:].bitcast(U8), LINE)
        en_s = keep.tile([P, N // 4], I32, name="en_s", tag="was", align_bytes=64)
        nc.gpsimd.memset(en_s[:], 0)
        load_scales((nc.sync,), en_s[:], 0, en_scales)

        pair = gather("g1_s01", U8, AT_G1_S01, tab1_s, list1, 0, 2 * CHUNK)
        g1_s[0] = pair[:, 0:CHUNK]
        g1_s[1] = pair[:, CHUNK:]
        g1_w[0] = gather("g1_w0", U32, AT_G1_W0, tab1_w, list1, 0, CHUNK)
        g1_w[1] = gather("g1_w1", U32, AT_G1_W1, tab1_w, list1, CHUNK, CHUNK)
        pair = gather("g1_s23", U8, AT_G1_S23, tab1_s, list1, 2 * CHUNK, 2 * CHUNK)
        g1_s[2] = pair[:, 0:CHUNK]
        g1_s[LAST] = pair[:, CHUNK:]
        for c in range(2):
            open_sum(c, 0)
            open_sum(c, 1)
        g2_w[0] = gather("g2_w0", U32, AT_G2_W0, tab2_w, list2, 0, CHUNK)
        g2_w[1] = gather("g2_w1", U32, AT_G2_W1, tab2_w, list2, CHUNK, CHUNK)
        g2_w[2] = gather("g2_w2", U32, AT_G2_W2, tab2_w, list2, 2 * CHUNK, CHUNK)
        g1_w[2] = gather("g1_w2", U32, AT_G1_W1 - 2 * CHUNK, tab1_w, list1, 2 * CHUNK, CHUNK)
        g1_w[LAST] = gather("g1_w3", U32, AT_G1_W1 + 2 * CHUNK, tab1_w, list1, LAST * CHUNK, CHUNK)

        for c in range(LAST):
            for s in range(2):
                if c == 2:
                    open_sum(c, s)
                close_sum(c, s)
                if s == 0:
                    h[c] = lay.tile([P, CHUNK, PACK], BF16, name="h%d" % c, align_bytes=64, offset=AT_H + c * H_STEP)
                nc.scalar.activation(out=h[c][:, s * PART : (s + 1) * PART, :], in_=interleaved(c, s), func=RELU)

        quantise(0, whole, h[0][:])
        y0 = banks.tile([P, 2, CHUNK], F32, name="y0", tag="bank4")
        for u in range(2):
            score(0, whole, u, y0[:, u, :])
        quantise_part(1, 0)
        open_sum(LAST, 0)
        y1a = score_part(1, 0, "yp1_0", 5)
        open_sum(LAST, 1)
        g2_w[LAST] = gather("g2_w3", U32, AT_G2_W2, tab2_w, list2, LAST * CHUNK, CHUNK)
        close_sum(LAST, 0)
        close_sum(LAST, 1)
        quantise_part(1, 1)
        y1b = score_part(1, 1, "yp1_1", 6)
        res0 = keep.tile([P, 2, CHUNK], F32, name="res0")
        nc.scalar.copy(res0[:], y0[:])
        nc.sync.dma_start(out=out.rearrange("(u p) j -> p u j", p=P)[:, :, 0:CHUNK], in_=res0[:])
        store_part(nc.scalar.copy, y1a, 1, 0, keep.tile([P, 2, PART], F32, name="res1a"))
        for s in range(2):
            quantise_part(2, s)
        y2 = []
        for u, bank in enumerate((7, 4)):
            y2.append(banks.tile([P, CHUNK], F32, name="y2_%d" % u, tag="bank%d" % bank))
            score(2, whole, u, y2[u][:])

        at_h2 = AT_H + 2 * H_STEP
        h_last = [
            lay.tile([P, PART, PACK], BF16, name="h3a", align_bytes=64, offset=at_h2),
            lay.tile([P, PART, PACK], BF16, name="h3b", align_bytes=64, offset=at_h2 + H_STEP),
        ]
        nc.vector.tensor_scalar_max(h_last[0][:], interleaved(LAST, 0), 0.0)
        nc.scalar.activation(out=h_last[1][:], in_=interleaved(LAST, 1), func=RELU)
        res1b = lay.tile([P, 2, PART], F32, name="res1b", align_bytes=64, offset=at_h2 + 2 * PACK * PART)
        store_part(nc.vector.tensor_copy, y1b, 1, 1, res1b)

        quantise(LAST, slice(0, PART), h_last[0][:])
        y3a = score_part(LAST, 0, "y3_0", 0)
        quantise(LAST, slice(PART, CHUNK), h_last[1][:])
        y3b = [banks.tile([P, PART], F32, name="y3_1%d" % u, tag="bank%d" % (1 + u)) for u in range(2)]
        for u in range(2):
            score(LAST, slice(PART, CHUNK), u, y3b[u][:])
        store_rows(y2[0][:], 2, 0, keep.tile([P, CHUNK], F32, name="res2a"))
        store_rows(y2[1][:], 2, 1, keep.tile([P, CHUNK], F32, name="res2b"))
        store_part(nc.vector.tensor_copy, y3a, LAST, 0, keep.tile([P, 2, PART], F32, name="res3"))
        for u, (copy, queue) in enumerate(((nc.vector.tensor_copy, nc.sync), (nc.scalar.copy, nc.scalar))):
            res = keep.tile([P, PART], F32, name="res4_%d" % u)
            copy(res[:], y3b[u][:])
            queue.dma_start(out=out[u * P : (u + 1) * P, J - PART : J], in_=res[:])
